import numpy as np
import ml_dtypes


def mxq(x, axis, fmt="e4m3"):
    dtype, down = {"e4m3": (ml_dtypes.float8_e4m3fn, 7), "e5m2": (ml_dtypes.float8_e5m2, 14)}[fmt]
    v = np.moveaxis(np.asarray(x, np.float32).astype(ml_dtypes.bfloat16).astype(np.float64), axis, -1)
    blocks = v.reshape(v.shape[:-1] + (-1, 32))
    amax = np.abs(blocks).max(-1, keepdims=True)
    byte = np.maximum(np.where(amax > 0, np.frexp(amax)[1] - 1 + 127, 0) - down, 1)
    scale = np.exp2(byte - 127.0)
    codes = (blocks / scale).astype(np.float32).astype(dtype).astype(np.float64)
    return np.moveaxis((codes * scale).reshape(v.shape), -1, axis)


WIDE = False


def mx_kscale(k):
    if not WIDE:
        return np.ones(k)
    levels = np.array([10, -10, 5, -5, 0])
    if k % 512:
        return np.exp2(np.random.permutation(np.resize(levels, k // 32))).repeat(32)
    a = np.empty((k // 512, 16))
    for p in range(k // 512):
        a[p, :8] = np.random.permutation(np.resize(levels, 8))
        for g in range(8):
            far = levels[np.abs(levels - a[p, g]) >= 10]
            a[p, g + 8] = far[np.random.randint(len(far))]
    return np.exp2(a.ravel()).repeat(32)


def f64(x):
    return np.asarray(x).astype(np.float64)


E2M1 = np.array([0.0, 0.5, 1.0, 1.5, 2.0, 3.0, 4.0, 6.0, -0.0, -0.5, -1.0, -1.5, -2.0, -3.0, -4.0, -6.0])


def pack_weight(w, fmt):
    k, n = w.shape
    w = f64(np.asarray(w, np.float32).astype(ml_dtypes.bfloat16)).reshape(k // 32, 32, n)
    amax = np.abs(w).max(1)
    if fmt == "e4m3":
        byte = np.frexp(amax)[1] - 1 + 127 - 7
    else:
        mant, ex = np.frexp(amax / 6.0)
        byte = np.where(mant > 0.5, ex, ex - 1) + 127
    byte = np.clip(np.where(amax > 0, byte, 1), 1, 254)
    scaled = (w * np.exp2(127.0 - byte)[:, None, :]).reshape(k, n).astype(np.float32)
    by_word = np.ascontiguousarray(scaled.reshape(k // 512, 128, 4, n).transpose(0, 1, 3, 2))
    if fmt == "e4m3":
        words = by_word.astype(ml_dtypes.float8_e4m3fn).view(np.uint8)
    else:
        c = by_word.astype(ml_dtypes.float4_e2m1fn).view(np.uint8) & 0xF
        words = (c[..., 0::2] | (c[..., 1::2] << 4)).reshape(k // 512, 128, 2 * n)
    return np.ascontiguousarray(words), np.ascontiguousarray(byte.astype(np.uint8).reshape(k // 512, 16, n))


def unpack_weight(words, scales, fmt):
    g, _, n = scales.shape
    words = np.ascontiguousarray(words).reshape(g, 128, n, -1)
    if fmt == "e4m3":
        vals = words.view(ml_dtypes.float8_e4m3fn).astype(np.float64)
    else:
        nib = np.empty((g, 128, n, 4), np.uint8)
        nib[..., 0::2] = words & 0xF
        nib[..., 1::2] = words >> 4
        vals = E2M1[nib]
    vals = vals * np.repeat(np.exp2(scales.astype(np.float64) - 127.0), 8, axis=1)[..., None]
    return vals.transpose(0, 1, 3, 2).reshape(g * 512, n)


def planes(y):
    n, m = y.shape
    v = y.astype(np.float32).astype(ml_dtypes.bfloat16).astype(np.float64).reshape(n // 32, 32, m)
    top = np.abs(v).max(1)
    byte = np.clip(np.where(top > 0, np.frexp(top)[1] - 1 + 127 - 7, 1), 1, 254)
    codes = (v * np.exp2(127.0 - byte)[:, None, :]).reshape(n, m).astype(np.float32).astype(ml_dtypes.float8_e4m3fn).view(np.uint8)
    words = codes.reshape(n // 512, 128, 4, m).transpose(0, 1, 3, 2)
    return np.ascontiguousarray(words), np.ascontiguousarray(byte.astype(np.uint8).reshape(n // 512, 16, m))


K, R, M, T = 1024, 512, 1024, 1024


def setup_inputs():
    n = np.random.standard_normal
    s = mx_kscale(K)[:, None]
    u = mx_kscale(R)[:, None]
    p_w4 = pack_weight(n((K, M)) / np.sqrt(K) / s, "e2m1")
    return {
        "x": (n((K, T)) * s).astype(np.float32),
        "w4_words": p_w4[0],
        "w4_scales": p_w4[1],
        "down": (n((K, R)) / np.sqrt(K) / s * u.T).astype(np.float32),
        "up": (0.5 * n((R, M)) / np.sqrt(R) / u).astype(np.float32),
    }


def reference(x, w4_words, w4_scales, down, up):
    x_ = mxq(f64(x), 0, "e4m3")
    w4_ = unpack_weight(w4_words, w4_scales, "e2m1")
    down_ = mxq(f64(down), 0, "e4m3")
    up_ = mxq(f64(up), 0, "e4m3")
    h_ = mxq(down_.T @ x_, 0, "e4m3")
    y = w4_.T @ x_ + up_.T @ h_
    out_0 = y
    return (out_0,) + planes(out_0)

@@ -1,0 +1,254 @@
+from contextlib import ExitStack
+
+import concourse.mybir as mybir
+
+K, R, M, T = 1024, 512, 1024, 1024
+FLOPS = 2 * T * (K * R + K * M + R * M)
+
+F32 = mybir.dt.float32
+BF16 = mybir.dt.bfloat16
+I32 = mybir.dt.int32
+U32 = mybir.dt.uint32
+U8 = mybir.dt.uint8
+FP8X4 = mybir.dt.float8_e4m3fn_x4
+FP4X4 = mybir.dt.float4_e2m1fn_x4
+
+P = 128
+PACK = 4
+KP = 512
+TC = 512
+SUB = 128
+V_SHARE = 80
+
+
+def tile_mix_lowrank_fm_pl_none_kernel(tc, x, w4_words, w4_scales, down, up, out_0, out_1, out_2):
+    nc = tc.nc
+    with ExitStack() as ctx:
+        sb = ctx.enter_context(tc.tile_pool(name="sb", bufs=1))
+        ps = ctx.enter_context(tc.psum_pool(name="ps", bufs=1))
+        ctx.enter_context(tc.manual_schedule())
+
+        def sbuf(name, shape, dtype):
+            return sb.tile(shape, dtype, name=name, align_bytes=64)
+
+        pairs = [(i, j) for i in range(2) for j in range(2)]
+        x_raw = {gc: sbuf("x_raw%d%d" % gc, [P, PACK, TC], F32) for gc in pairs}
+        x_bf = {gc: sbuf("x_bf%d%d" % gc, [P, TC, PACK], BF16) for gc in pairs}
+        x_codes = {gc: sbuf("x_codes%d%d" % gc, [P, TC], U32) for gc in pairs}
+        x_scales = {gc: sbuf("x_scales%d%d" % gc, [P, TC], U8) for gc in pairs}
+        names = ["down0", "down1", "up0", "up1"]
+        w_raw = {n: sbuf(n + "_raw", [P, PACK, KP], F32) for n in names}
+        w_bf = {n: sbuf(n + "_bf", [P, PACK, P, PACK], BF16) for n in names}
+        w_codes = {n: sbuf(n + "_codes", [P, KP], U32) for n in names}
+        w_scales = {n: sbuf(n + "_scales", [P, KP], U8) for n in names}
+        w4_raw = sbuf("w4_raw", [P, 2, 2 * M], U8)
+        w4_dealt = sbuf("w4_dealt", [P, 2, 2 * M], U8)
+        s4_raw = sbuf("s4_raw", [P, 2, M], U8)
+        s4_dealt = sbuf("s4_dealt", [P, 2, M], U8)
+        h_bf = [sbuf("h_bf%d" % c, [P, TC, PACK], BF16) for c in range(2)]
+        h_codes = [sbuf("h_codes%d" % c, [P, TC], U32) for c in range(2)]
+        h_scales = [sbuf("h_scales%d" % c, [P, TC], U8) for c in range(2)]
+        y_f32 = {ac: sbuf("y_f32%d%d" % ac, [P, PACK, TC], F32) for ac in pairs}
+        y_bf = {ac: sbuf("y_bf%d%d" % ac, [P, TC, PACK], BF16) for ac in pairs}
+        y_codes = {ac: sbuf("y_codes%d%d" % ac, [P, TC], U32) for ac in pairs}
+        y_scales = [sbuf("y_scales%d" % c, [P, 2, TC], U8) for c in range(2)]
+
+        def copy(eng, out, in_):
+            if eng is nc.scalar:
+                nc.scalar.copy(out=out, in_=in_)
+            else:
+                nc.vector.tensor_copy(out=out, in_=in_)
+
+        def load_x(g, c):
+            rows = x[g * KP:(g + 1) * KP, c * TC:(c + 1) * TC]
+            nc.sync.dma_start(out=x_raw[g, c][:], in_=rows.rearrange("(p j) t -> p j t", j=PACK))
+
+        def load_w(name, rows):
+            nc.sync.dma_start(out=w_raw[name][:], in_=rows.rearrange("(p j) n -> p j n", j=PACK))
+
+        def interleave(eng, dst, src, lo, hi):
+            copy(eng,
+                 dst[:, lo:hi, :].rearrange("p (c i) j -> p c j i", i=4),
+                 src[:, :, lo:hi].rearrange("p j (c i) -> p c j i", i=4))
+
+        def deal(eng, name, lo, hi):
+            copy(eng,
+                 w_bf[name][:, :, lo:hi, :].rearrange("p r m j -> p m j r"),
+                 w_raw[name][:, :, PACK * lo:PACK * hi].rearrange("p j (m r) -> p m j r", r=PACK))
+
+        def quantize(codes, scales, flat, lo, hi):
+            nc.vector.quantize_mx(out=codes[:, lo:hi].bitcast(FP8X4), scales=scales[:, lo:hi],
+                                  in_=flat[:, PACK * lo:PACK * hi])
+
+        def quant_x(g, c, lo=0, hi=TC):
+            quantize(x_codes[g, c], x_scales[g, c], x_bf[g, c][:].rearrange("p t j -> p (t j)"), lo, hi)
+
+        def quant_w(name, lo=0, hi=KP):
+            quantize(w_codes[name], w_scales[name], w_bf[name][:].rearrange("p r m j -> p (r m j)"), lo, hi)
+
+        def quant_h(c, lo, hi):
+            quantize(h_codes[c], h_scales[c], h_bf[c][:].rearrange("p t j -> p (t j)"), lo, hi)
+
+        def quant_y(a, c):
+            quantize(y_codes[a, c], y_scales[c][:, a, :], y_bf[a, c][:].rearrange("p t j -> p (t j)"), 0, TC)
+
+        acc = {}
+
+        def open_y(a, c, r, bank):
+            acc[a, c, r] = ps.tile([P, TC], F32, name="bank%d" % bank)
+
+        def base(a, c, r, g):
+            col = (a * PACK + r) * P
+            nc.tensor.matmul_mx(out=acc[a, c, r][:],
+                                lhsT=w4_dealt[:, g, 2 * col:2 * col + 2 * P].bitcast(FP4X4),
+                                lhsT_scale=s4_dealt[:, g, col:col + P],
+                                rhs=x_codes[g, c][:].bitcast(FP8X4), rhs_scale=x_scales[g, c][:],
+                                start=(g == 0), stop=False)
+
+        def branch(a, c, r):
+            name = "up%d" % a
+            nc.tensor.matmul_mx(out=acc[a, c, r][:],
+                                lhsT=w_codes[name][:, r * P:(r + 1) * P].bitcast(FP8X4),
+                                lhsT_scale=w_scales[name][:, r * P:(r + 1) * P],
+                                rhs=h_codes[c][:].bitcast(FP8X4), rhs_scale=h_scales[c][:],
+                                start=False, stop=True)
+
+        def make_h(c, s, bank):
+            cols = slice(s * SUB, (s + 1) * SUB)
+            h_acc = ps.tile([P, PACK, SUB], F32, name="bank%d" % bank)
+            for r in range(PACK):
+                for g in range(2):
+                    name = "down%d" % g
+                    nc.tensor.matmul_mx(out=h_acc[:, r, :],
+                                        lhsT=w_codes[name][:, r * P:(r + 1) * P].bitcast(FP8X4),
+                                        lhsT_scale=w_scales[name][:, r * P:(r + 1) * P],
+                                        rhs=x_codes[g, c][:, cols].bitcast(FP8X4), rhs_scale=x_scales[g, c][:, cols],
+                                        start=(g == 0), stop=(g == 1))
+            nc.scalar.copy(out=h_bf[c][:, cols, :], in_=h_acc[:].rearrange("p r t -> p t r"))
+
+        def drain(eng, a, c, r):
+            copy(eng, y_f32[a, c][:, r, :], acc[a, c, r][:])
+
+        def store_y(a, c, r_lo, r_hi):
+            rows = out_0[a * KP:(a + 1) * KP, c * TC:(c + 1) * TC].rearrange("(p r) t -> p r t", r=PACK)
+            nc.sync.dma_start(out=rows[:, r_lo:r_hi, :], in_=y_f32[a, c][:, r_lo:r_hi, :])
+
+        def store_codes(a, c):
+            words = out_1[a].rearrange("p t i -> p (t i)").bitcast(I32)
+            nc.sync.dma_start(out=words[:, c * TC:(c + 1) * TC], in_=y_codes[a, c][:].bitcast(I32))
+
+        def store_scales(eng, c):
+            for q in range(4):
+                rows = out_2[:, 4 * q:4 * q + 4, c * TC:(c + 1) * TC].rearrange("a r t -> r a t")
+                eng.dma_start(out=rows.bitcast(I32), in_=y_scales[c][32 * q:32 * q + 4, :, :].bitcast(I32))
+
+        nc.vector.memset(s4_raw[:].rearrange("p g n -> p (g n)").bitcast(I32), 0)
+        nc.sync.dma_start(out=w4_raw[:].bitcast(I32), in_=w4_words.rearrange("g p b -> p g b").bitcast(I32))
+        for q in range(4):
+            nc.sync.dma_start(out=s4_raw[32 * q:32 * q + 4, :, :].bitcast(I32),
+                              in_=w4_scales[:, 4 * q:4 * q + 4, :].rearrange("g r n -> r g n").bitcast(I32))
+        load_x(0, 0)
+        load_x(1, 0)
+        load_w("down0", down[0:KP, :])
+        load_w("down1", down[KP:2 * KP, :])
+        load_w("up0", up[:, 0:KP])
+        load_w("up1", up[:, KP:2 * KP])
+        load_x(0, 1)
+        load_x(1, 1)
+
+        for g, a in pairs:
+            cols = slice(a * 2 * KP, (a + 1) * 2 * KP)
+            nc.vector.tensor_copy(out=w4_dealt[:, g, cols].rearrange("p (r m b) -> p r m b", r=PACK, b=2),
+                                  in_=w4_raw[:, g, cols].rearrange("p (m r b) -> p r m b", r=PACK, b=2))
+        for g in range(2):
+            nc.vector.tensor_copy(out=s4_dealt[:, g, :].rearrange("p (a r m) -> p a r m", a=2, r=PACK),
+                                  in_=s4_raw[:, g, :].rearrange("p (a m r) -> p a r m", a=2, r=PACK))
+
+        interleave(nc.scalar, x_bf[0, 0], x_raw[0, 0], 0, TC)
+        interleave(nc.vector, x_bf[1, 0], x_raw[1, 0], 0, TC)
+        quant_x(0, 0)
+        quant_x(1, 0)
+        early = [(0, 0, r) for r in range(4)] + [(1, 0, 0), (1, 0, 1)]
+        for bank, key in enumerate(early):
+            open_y(*key, bank)
+            base(*key, 0)
+        for key in early:
+            base(*key, 1)
+        deal(nc.scalar, "down0", 64, P)
+        deal(nc.vector, "down0", 0, 64)
+        quant_w("down0")
+        deal(nc.scalar, "down1", V_SHARE, P)
+        deal(nc.vector, "down1", 0, V_SHARE)
+        for r in range(PACK):
+            quant_w("down1", r * P, (r + 1) * P)
+        for s in range(4):
+            make_h(0, s, 6 + s % 2)
+        deal(nc.vector, "up0", 0, P)
+        quant_h(0, 0, 256)
+        quant_w("up0")
+        quant_h(0, 256, 512)
+        for r in (2, 3):
+            open_y(1, 0, r, 4 + r)
+            base(1, 0, r, 0)
+            base(1, 0, r, 1)
+        deal(nc.scalar, "up1", V_SHARE, P)
+        deal(nc.vector, "up1", 0, V_SHARE)
+        for r in range(PACK):
+            branch(0, 0, r)
+            drain(nc.scalar, 0, 0, r)
+        store_y(0, 0, 0, 4)
+        quant_w("up1")
+        for r in range(PACK):
+            branch(1, 0, r)
+            drain(nc.scalar, 1, 0, r)
+        store_y(1, 0, 0, 4)
+
+        interleave(nc.vector, x_bf[0, 1], x_raw[0, 1], 0, TC)
+        quant_x(0, 1)
+        late = [(0, 1, r) for r in range(4)] + [(1, 1, 0), (1, 1, 1)]
+        for bank, key in enumerate(late):
+            open_y(*key, 2 + bank)
+            base(*key, 0)
+        interleave(nc.scalar, x_bf[1, 1], x_raw[1, 1], 3 * SUB, 4 * SUB)
+        interleave(nc.vector, x_bf[1, 1], x_raw[1, 1], 0, SUB)
+        interleave(nc.vector, x_bf[1, 1], x_raw[1, 1], SUB, 2 * SUB)
+        quant_x(1, 1, 0, SUB)
+        interleave(nc.vector, x_bf[1, 1], x_raw[1, 1], 2 * SUB, 3 * SUB)
+        quant_x(1, 1, SUB, 2 * SUB)
+        quant_x(1, 1, 2 * SUB, 3 * SUB)
+        quant_x(1, 1, 3 * SUB, 4 * SUB)
+        for s in range(4):
+            make_h(1, s, s % 2)
+        interleave(nc.vector, y_bf[0, 0], y_f32[0, 0], 0, TC)
+        quant_h(1, 0, 256)
+        quant_y(0, 0)
+        store_codes(0, 0)
+        quant_h(1, 256, 512)
+        for r in range(PACK):
+            base(0, 1, r, 1)
+        for r in range(PACK):
+            branch(0, 1, r)
+            drain(nc.scalar, 0, 1, r)
+            if r % 2:
+                store_y(0, 1, r - 1, r + 1)
+        interleave(nc.vector, y_bf[1, 0], y_f32[1, 0], 0, TC)
+        quant_y(1, 0)
+        store_codes(1, 0)
+        store_scales(nc.sync, 0)
+        for r in range(PACK):
+            if r >= 2:
+                open_y(1, 1, r, r - 2)
+                base(1, 1, r, 0)
+            base(1, 1, r, 1)
+            branch(1, 1, r)
+            drain(nc.scalar, 1, 1, r)
+            if r % 2:
+                store_y(1, 1, r - 1, r + 1)
+        interleave(nc.vector, y_bf[0, 1], y_f32[0, 1], 0, TC)
+        quant_y(0, 1)
+        store_codes(0, 1)
+        interleave(nc.scalar, y_bf[1, 1], y_f32[1, 1], 3 * SUB, TC)
+        interleave(nc.vector, y_bf[1, 1], y_f32[1, 1], 0, 3 * SUB)
+        quant_y(1, 1)
+        store_codes(1, 1)
+        store_scales(nc.scalar, 1)

@@ -15,14 +15,19 @@ FP4X4 = mybir.dt.float4_e2m1fn_x4
 
 P = 128
 PACK = 4
-KP = 512
-TC = 512
-SUB = 128
-V_SHARE = 80
+SPAN = P * PACK
+HALF = 512
+STRIP = 128
+QUAD = 32
+
+DEAL_CUT = 80
+X_CUT = 384
+Y_CUT = 320
 
 
 def tile_mix_lowrank_fm_pl_none_kernel(tc, x, w4_words, w4_scales, down, up, out_0, out_1, out_2):
     nc = tc.nc
+    scalar, vector = nc.scalar, nc.vector
     with ExitStack() as ctx:
         sb = ctx.enter_context(tc.tile_pool(name="sb", bufs=1))
         ps = ctx.enter_context(tc.psum_pool(name="ps", bufs=1))
@@ -31,224 +36,246 @@ def tile_mix_lowrank_fm_pl_none_kernel(tc, x, w4_words, w4_scales, down, up, out
         def sbuf(name, shape, dtype):
             return sb.tile(shape, dtype, name=name, align_bytes=64)
 
-        pairs = [(i, j) for i in range(2) for j in range(2)]
-        x_raw = {gc: sbuf("x_raw%d%d" % gc, [P, PACK, TC], F32) for gc in pairs}
-        x_bf = {gc: sbuf("x_bf%d%d" % gc, [P, TC, PACK], BF16) for gc in pairs}
-        x_codes = {gc: sbuf("x_codes%d%d" % gc, [P, TC], U32) for gc in pairs}
-        x_scales = {gc: sbuf("x_scales%d%d" % gc, [P, TC], U8) for gc in pairs}
-        names = ["down0", "down1", "up0", "up1"]
-        w_raw = {n: sbuf(n + "_raw", [P, PACK, KP], F32) for n in names}
-        w_bf = {n: sbuf(n + "_bf", [P, PACK, P, PACK], BF16) for n in names}
-        w_codes = {n: sbuf(n + "_codes", [P, KP], U32) for n in names}
-        w_scales = {n: sbuf(n + "_scales", [P, KP], U8) for n in names}
+        two_by_two = [(i, j) for i in range(2) for j in range(2)]
+        x_raw = {gc: sbuf("x_raw%d%d" % gc, [P, PACK, HALF], F32) for gc in two_by_two}
+        x_bf = {gc: sbuf("x_bf%d%d" % gc, [P, HALF, PACK], BF16) for gc in two_by_two}
+        x_codes = {gc: sbuf("x_codes%d%d" % gc, [P, HALF], U32) for gc in two_by_two}
+        x_scales = {gc: sbuf("x_scales%d%d" % gc, [P, HALF], U8) for gc in two_by_two}
+        pieces = {"down0": down[:SPAN, :], "down1": down[SPAN:, :], "up0": up[:, :SPAN], "up1": up[:, SPAN:]}
+        w_raw = {name: sbuf(name + "_raw", [P, PACK, SPAN], F32) for name in pieces}
+        w_bf = {name: sbuf(name + "_bf", [P, PACK, P, PACK], BF16) for name in pieces}
+        w_codes = {name: sbuf(name + "_codes", [P, SPAN], U32) for name in pieces}
+        w_scales = {name: sbuf(name + "_scales", [P, SPAN], U8) for name in pieces}
         w4_raw = sbuf("w4_raw", [P, 2, 2 * M], U8)
         w4_dealt = sbuf("w4_dealt", [P, 2, 2 * M], U8)
         s4_raw = sbuf("s4_raw", [P, 2, M], U8)
         s4_dealt = sbuf("s4_dealt", [P, 2, M], U8)
-        h_bf = [sbuf("h_bf%d" % c, [P, TC, PACK], BF16) for c in range(2)]
-        h_codes = [sbuf("h_codes%d" % c, [P, TC], U32) for c in range(2)]
-        h_scales = [sbuf("h_scales%d" % c, [P, TC], U8) for c in range(2)]
-        y_f32 = {ac: sbuf("y_f32%d%d" % ac, [P, PACK, TC], F32) for ac in pairs}
-        y_bf = {ac: sbuf("y_bf%d%d" % ac, [P, TC, PACK], BF16) for ac in pairs}
-        y_codes = {ac: sbuf("y_codes%d%d" % ac, [P, TC], U32) for ac in pairs}
-        y_scales = [sbuf("y_scales%d" % c, [P, 2, TC], U8) for c in range(2)]
+        h_bf = [sbuf("h_bf%d" % c, [P, HALF, PACK], BF16) for c in range(2)]
+        h_codes = [sbuf("h_codes%d" % c, [P, HALF], U32) for c in range(2)]
+        h_scales = [sbuf("h_scales%d" % c, [P, HALF], U8) for c in range(2)]
+        y_f32 = {ac: sbuf("y_f32%d%d" % ac, [P, PACK, HALF], F32) for ac in two_by_two}
+        y_bf = {ac: sbuf("y_bf%d%d" % ac, [P, HALF, PACK], BF16) for ac in two_by_two}
+        y_codes = {ac: sbuf("y_codes%d%d" % ac, [P, HALF], U32) for ac in two_by_two}
+        y_scales = [sbuf("y_scales%d" % c, [P, 2, HALF], U8) for c in range(2)]
+        y_acc = {}
 
-        def copy(eng, out, in_):
-            if eng is nc.scalar:
-                nc.scalar.copy(out=out, in_=in_)
+        def copy(engine, out, in_):
+            if engine is scalar:
+                scalar.copy(out=out, in_=in_)
             else:
-                nc.vector.tensor_copy(out=out, in_=in_)
+                vector.tensor_copy(out=out, in_=in_)
 
-        def load_x(g, c):
-            rows = x[g * KP:(g + 1) * KP, c * TC:(c + 1) * TC]
-            nc.sync.dma_start(out=x_raw[g, c][:], in_=rows.rearrange("(p j) t -> p j t", j=PACK))
+        def load_x(g, c, lo=0, hi=HALF):
+            rows = x[g * SPAN:(g + 1) * SPAN, c * HALF + lo:c * HALF + hi]
+            nc.sync.dma_start(out=x_raw[g, c][:, :, lo:hi], in_=rows.rearrange("(p j) t -> p j t", j=PACK))
 
-        def load_w(name, rows):
-            nc.sync.dma_start(out=w_raw[name][:], in_=rows.rearrange("(p j) n -> p j n", j=PACK))
+        def load_w(name):
+            nc.sync.dma_start(out=w_raw[name][:], in_=pieces[name].rearrange("(p j) n -> p j n", j=PACK))
 
-        def interleave(eng, dst, src, lo, hi):
-            copy(eng,
-                 dst[:, lo:hi, :].rearrange("p (c i) j -> p c j i", i=4),
-                 src[:, :, lo:hi].rearrange("p j (c i) -> p c j i", i=4))
+        def interleave(engine, dst, src, lo, hi):
+            copy(engine,
+                 dst[:, lo:hi, :].rearrange("p (u i) j -> p u j i", i=4),
+                 src[:, :, lo:hi].rearrange("p j (u i) -> p u j i", i=4))
 
-        def deal(eng, name, lo, hi):
-            copy(eng,
-                 w_bf[name][:, :, lo:hi, :].rearrange("p r m j -> p m j r"),
-                 w_raw[name][:, :, PACK * lo:PACK * hi].rearrange("p j (m r) -> p m j r", r=PACK))
+        def cast_x(engine, g, c, lo, hi):
+            interleave(engine, x_bf[g, c], x_raw[g, c], lo, hi)
 
-        def quantize(codes, scales, flat, lo, hi):
-            nc.vector.quantize_mx(out=codes[:, lo:hi].bitcast(FP8X4), scales=scales[:, lo:hi],
-                                  in_=flat[:, PACK * lo:PACK * hi])
+        def cast_y(engine, a, c, lo=0, hi=HALF):
+            interleave(engine, y_bf[a, c], y_f32[a, c], lo, hi)
 
-        def quant_x(g, c, lo=0, hi=TC):
+        def cast_w(engine, name, lo, hi):
+            copy(engine,
+                 w_bf[name][:, :, lo:hi, :].rearrange("p s m j -> p m j s"),
+                 w_raw[name][:, :, PACK * lo:PACK * hi].rearrange("p j (m s) -> p m j s", s=PACK))
+
+        def cast_w_shared(name):
+            cast_w(vector, name, 0, DEAL_CUT)
+            cast_w(scalar, name, DEAL_CUT, P)
+
+        def quantize(codes, scales, values, lo, hi):
+            vector.quantize_mx(out=codes[:, lo:hi].bitcast(FP8X4), scales=scales[:, lo:hi],
+                               in_=values[:, PACK * lo:PACK * hi])
+
+        def quant_x(g, c, lo=0, hi=HALF):
             quantize(x_codes[g, c], x_scales[g, c], x_bf[g, c][:].rearrange("p t j -> p (t j)"), lo, hi)
 
-        def quant_w(name, lo=0, hi=KP):
-            quantize(w_codes[name], w_scales[name], w_bf[name][:].rearrange("p r m j -> p (r m j)"), lo, hi)
+        def quant_w(name):
+            quantize(w_codes[name], w_scales[name], w_bf[name][:].rearrange("p s m j -> p (s m j)"), 0, SPAN)
 
         def quant_h(c, lo, hi):
             quantize(h_codes[c], h_scales[c], h_bf[c][:].rearrange("p t j -> p (t j)"), lo, hi)
 
-        def quant_y(a, c):
-            quantize(y_codes[a, c], y_scales[c][:, a, :], y_bf[a, c][:].rearrange("p t j -> p (t j)"), 0, TC)
+        def quant_y(a, c, lo=0, hi=HALF):
+            quantize(y_codes[a, c], y_scales[c][:, a, :], y_bf[a, c][:].rearrange("p t j -> p (t j)"), lo, hi)
 
-        acc = {}
+        def strip(i):
+            return i * STRIP, (i + 1) * STRIP
 
-        def open_y(a, c, r, bank):
-            acc[a, c, r] = ps.tile([P, TC], F32, name="bank%d" % bank)
-
-        def base(a, c, r, g):
-            col = (a * PACK + r) * P
-            nc.tensor.matmul_mx(out=acc[a, c, r][:],
-                                lhsT=w4_dealt[:, g, 2 * col:2 * col + 2 * P].bitcast(FP4X4),
+        def base(a, c, s, g):
+            col = a * SPAN + s * P
+            nc.tensor.matmul_mx(out=y_acc[a, c, s][:],
+                                lhsT=w4_dealt[:, g, 2 * col:2 * (col + P)].bitcast(FP4X4),
                                 lhsT_scale=s4_dealt[:, g, col:col + P],
                                 rhs=x_codes[g, c][:].bitcast(FP8X4), rhs_scale=x_scales[g, c][:],
                                 start=(g == 0), stop=False)
 
-        def branch(a, c, r):
+        def open_y(a, c, s, bank):
+            y_acc[a, c, s] = ps.tile([P, HALF], F32, name="bank%d" % bank)
+            base(a, c, s, 0)
+
+        def branch(a, c, s):
             name = "up%d" % a
-            nc.tensor.matmul_mx(out=acc[a, c, r][:],
-                                lhsT=w_codes[name][:, r * P:(r + 1) * P].bitcast(FP8X4),
-                                lhsT_scale=w_scales[name][:, r * P:(r + 1) * P],
+            nc.tensor.matmul_mx(out=y_acc[a, c, s][:],
+                                lhsT=w_codes[name][:, s * P:(s + 1) * P].bitcast(FP8X4),
+                                lhsT_scale=w_scales[name][:, s * P:(s + 1) * P],
                                 rhs=h_codes[c][:].bitcast(FP8X4), rhs_scale=h_scales[c][:],
                                 start=False, stop=True)
 
-        def make_h(c, s, bank):
-            cols = slice(s * SUB, (s + 1) * SUB)
-            h_acc = ps.tile([P, PACK, SUB], F32, name="bank%d" % bank)
-            for r in range(PACK):
+        def make_h(c, i, bank):
+            cols = slice(*strip(i))
+            h_acc = ps.tile([P, PACK, STRIP], F32, name="bank%d" % bank)
+            for s in range(PACK):
                 for g in range(2):
                     name = "down%d" % g
-                    nc.tensor.matmul_mx(out=h_acc[:, r, :],
-                                        lhsT=w_codes[name][:, r * P:(r + 1) * P].bitcast(FP8X4),
-                                        lhsT_scale=w_scales[name][:, r * P:(r + 1) * P],
+                    nc.tensor.matmul_mx(out=h_acc[:, s, :],
+                                        lhsT=w_codes[name][:, s * P:(s + 1) * P].bitcast(FP8X4),
+                                        lhsT_scale=w_scales[name][:, s * P:(s + 1) * P],
                                         rhs=x_codes[g, c][:, cols].bitcast(FP8X4), rhs_scale=x_scales[g, c][:, cols],
                                         start=(g == 0), stop=(g == 1))
-            nc.scalar.copy(out=h_bf[c][:, cols, :], in_=h_acc[:].rearrange("p r t -> p t r"))
+            scalar.copy(out=h_bf[c][:, cols, :], in_=h_acc[:].rearrange("p s t -> p t s"))
 
-        def drain(eng, a, c, r):
-            copy(eng, y_f32[a, c][:, r, :], acc[a, c, r][:])
+        def drain(engine, a, c, s, lo=0, hi=HALF):
+            copy(engine, y_f32[a, c][:, s, lo:hi], y_acc[a, c, s][:, lo:hi])
 
-        def store_y(a, c, r_lo, r_hi):
-            rows = out_0[a * KP:(a + 1) * KP, c * TC:(c + 1) * TC].rearrange("(p r) t -> p r t", r=PACK)
-            nc.sync.dma_start(out=rows[:, r_lo:r_hi, :], in_=y_f32[a, c][:, r_lo:r_hi, :])
+        def store_y(a, c, s):
+            rows = out_0[a * SPAN:(a + 1) * SPAN, c * HALF:(c + 1) * HALF].rearrange("(p s) t -> p s t", s=PACK)
+            nc.sync.dma_start(out=rows[:, s:s + 2, :], in_=y_f32[a, c][:, s:s + 2, :])
 
         def store_codes(a, c):
-            words = out_1[a].rearrange("p t i -> p (t i)").bitcast(I32)
-            nc.sync.dma_start(out=words[:, c * TC:(c + 1) * TC], in_=y_codes[a, c][:].bitcast(I32))
+            words = out_1[a].rearrange("p t j -> p (t j)").bitcast(I32)
+            nc.sync.dma_start(out=words[:, c * HALF:(c + 1) * HALF], in_=y_codes[a, c][:].bitcast(I32))
 
-        def store_scales(eng, c):
-            for q in range(4):
-                rows = out_2[:, 4 * q:4 * q + 4, c * TC:(c + 1) * TC].rearrange("a r t -> r a t")
-                eng.dma_start(out=rows.bitcast(I32), in_=y_scales[c][32 * q:32 * q + 4, :, :].bitcast(I32))
+        def store_scales(c):
+            for quad in range(PACK):
+                rows = out_2[:, 4 * quad:4 * quad + 4, c * HALF:(c + 1) * HALF].rearrange("a q t -> q a t")
+                nc.sync.dma_start(out=rows.bitcast(I32),
+                                  in_=y_scales[c][QUAD * quad:QUAD * quad + 4, :, :].bitcast(I32))
 
-        nc.vector.memset(s4_raw[:].rearrange("p g n -> p (g n)").bitcast(I32), 0)
+        vector.memset(s4_raw[:].rearrange("p g n -> p (g n)").bitcast(I32), 0)
         nc.sync.dma_start(out=w4_raw[:].bitcast(I32), in_=w4_words.rearrange("g p b -> p g b").bitcast(I32))
-        for q in range(4):
-            nc.sync.dma_start(out=s4_raw[32 * q:32 * q + 4, :, :].bitcast(I32),
-                              in_=w4_scales[:, 4 * q:4 * q + 4, :].rearrange("g r n -> r g n").bitcast(I32))
+        for quad in range(PACK):
+            nc.sync.dma_start(out=s4_raw[QUAD * quad:QUAD * quad + 4, :, :].bitcast(I32),
+                              in_=w4_scales[:, 4 * quad:4 * quad + 4, :].rearrange("g q n -> q g n").bitcast(I32))
         load_x(0, 0)
+        load_w("down0")
+        load_w("down1")
         load_x(1, 0)
-        load_w("down0", down[0:KP, :])
-        load_w("down1", down[KP:2 * KP, :])
-        load_w("up0", up[:, 0:KP])
-        load_w("up1", up[:, KP:2 * KP])
+        load_w("up0")
+        load_w("up1")
         load_x(0, 1)
-        load_x(1, 1)
+        load_x(1, 1, 0, HALF // 2)
+        load_x(1, 1, HALF // 2, HALF)
 
-        for g, a in pairs:
-            cols = slice(a * 2 * KP, (a + 1) * 2 * KP)
-            nc.vector.tensor_copy(out=w4_dealt[:, g, cols].rearrange("p (r m b) -> p r m b", r=PACK, b=2),
-                                  in_=w4_raw[:, g, cols].rearrange("p (m r b) -> p r m b", r=PACK, b=2))
+        for g, a in two_by_two:
+            cols = slice(2 * a * SPAN, 2 * (a + 1) * SPAN)
+            vector.tensor_copy(out=w4_dealt[:, g, cols].rearrange("p (s m b) -> p s m b", s=PACK, b=2),
+                               in_=w4_raw[:, g, cols].rearrange("p (m s b) -> p s m b", s=PACK, b=2))
         for g in range(2):
-            nc.vector.tensor_copy(out=s4_dealt[:, g, :].rearrange("p (a r m) -> p a r m", a=2, r=PACK),
-                                  in_=s4_raw[:, g, :].rearrange("p (a m r) -> p a r m", a=2, r=PACK))
+            vector.tensor_copy(out=s4_dealt[:, g, :].rearrange("p (a s m) -> p a s m", a=2, s=PACK),
+                               in_=s4_raw[:, g, :].rearrange("p (a m s) -> p a s m", a=2, s=PACK))
 
-        interleave(nc.scalar, x_bf[0, 0], x_raw[0, 0], 0, TC)
-        interleave(nc.vector, x_bf[1, 0], x_raw[1, 0], 0, TC)
+        cast_x(vector, 0, 0, 0, X_CUT)
+        cast_x(scalar, 0, 0, X_CUT, HALF)
+        cast_w_shared("down0")
+        quant_w("down0")
         quant_x(0, 0)
-        quant_x(1, 0)
-        early = [(0, 0, r) for r in range(4)] + [(1, 0, 0), (1, 0, 1)]
+        early = [(0, 0, s) for s in range(PACK)] + [(1, 0, 0)]
         for bank, key in enumerate(early):
             open_y(*key, bank)
-            base(*key, 0)
+        cast_w_shared("down1")
+        quant_w("down1")
+        for i in range(PACK):
+            cast_x(vector if i < 2 else scalar, 1, 0, *strip(i))
+        for i in range(PACK):
+            quant_x(1, 0, *strip(i))
+        for i, bank in enumerate((5, 6, 7, 5)):
+            make_h(0, i, bank)
+        cast_w(vector, "up0", 0, P)
+        quant_h(0, 0, HALF // 2)
+        quant_w("up0")
+        quant_h(0, HALF // 2, HALF)
+        cast_w_shared("up1")
+        quant_w("up1")
         for key in early:
             base(*key, 1)
-        deal(nc.scalar, "down0", 64, P)
-        deal(nc.vector, "down0", 0, 64)
-        quant_w("down0")
-        deal(nc.scalar, "down1", V_SHARE, P)
-        deal(nc.vector, "down1", 0, V_SHARE)
-        for r in range(PACK):
-            quant_w("down1", r * P, (r + 1) * P)
-        for s in range(4):
-            make_h(0, s, 6 + s % 2)
-        deal(nc.vector, "up0", 0, P)
-        quant_h(0, 0, 256)
-        quant_w("up0")
-        quant_h(0, 256, 512)
-        for r in (2, 3):
-            open_y(1, 0, r, 4 + r)
-            base(1, 0, r, 0)
-            base(1, 0, r, 1)
-        deal(nc.scalar, "up1", V_SHARE, P)
-        deal(nc.vector, "up1", 0, V_SHARE)
-        for r in range(PACK):
-            branch(0, 0, r)
-            drain(nc.scalar, 0, 0, r)
-        store_y(0, 0, 0, 4)
-        quant_w("up1")
-        for r in range(PACK):
-            branch(1, 0, r)
-            drain(nc.scalar, 1, 0, r)
-        store_y(1, 0, 0, 4)
+        open_y(1, 0, 1, 6)
+        base(1, 0, 1, 1)
+        for s in range(PACK):
+            branch(0, 0, s)
+        for s, bank in ((2, 7), (3, 5)):
+            open_y(1, 0, s, bank)
+            base(1, 0, s, 1)
+        for s in range(PACK):
+            branch(1, 0, s)
+        drain(scalar, 0, 0, 0)
+        drain(scalar, 0, 0, 1)
+        store_y(0, 0, 0)
+        cast_x(vector, 0, 1, 0, X_CUT)
+        cast_x(scalar, 0, 1, X_CUT, HALF)
+        for a, s in ((0, 2), (1, 0), (1, 2)):
+            drain(scalar, a, 0, s)
+            drain(scalar, a, 0, s + 1)
+            store_y(a, 0, s)
 
-        interleave(nc.vector, x_bf[0, 1], x_raw[0, 1], 0, TC)
-        quant_x(0, 1)
-        late = [(0, 1, r) for r in range(4)] + [(1, 1, 0), (1, 1, 1)]
-        for bank, key in enumerate(late):
-            open_y(*key, 2 + bank)
-            base(*key, 0)
-        interleave(nc.scalar, x_bf[1, 1], x_raw[1, 1], 3 * SUB, 4 * SUB)
-        interleave(nc.vector, x_bf[1, 1], x_raw[1, 1], 0, SUB)
-        interleave(nc.vector, x_bf[1, 1], x_raw[1, 1], SUB, 2 * SUB)
-        quant_x(1, 1, 0, SUB)
-        interleave(nc.vector, x_bf[1, 1], x_raw[1, 1], 2 * SUB, 3 * SUB)
-        quant_x(1, 1, SUB, 2 * SUB)
-        quant_x(1, 1, 2 * SUB, 3 * SUB)
-        quant_x(1, 1, 3 * SUB, 4 * SUB)
-        for s in range(4):
-            make_h(1, s, s % 2)
-        interleave(nc.vector, y_bf[0, 0], y_f32[0, 0], 0, TC)
-        quant_h(1, 0, 256)
-        quant_y(0, 0)
-        store_codes(0, 0)
-        quant_h(1, 256, 512)
-        for r in range(PACK):
-            base(0, 1, r, 1)
-        for r in range(PACK):
-            branch(0, 1, r)
-            drain(nc.scalar, 0, 1, r)
-            if r % 2:
-                store_y(0, 1, r - 1, r + 1)
-        interleave(nc.vector, y_bf[1, 0], y_f32[1, 0], 0, TC)
-        quant_y(1, 0)
-        store_codes(1, 0)
-        store_scales(nc.sync, 0)
-        for r in range(PACK):
-            if r >= 2:
-                open_y(1, 1, r, r - 2)
-                base(1, 1, r, 0)
-            base(1, 1, r, 1)
-            branch(1, 1, r)
-            drain(nc.scalar, 1, 1, r)
-            if r % 2:
-                store_y(1, 1, r - 1, r + 1)
-        interleave(nc.vector, y_bf[0, 1], y_f32[0, 1], 0, TC)
+        quant_x(0, 1, 0, HALF // 2)
+        quant_x(0, 1, HALF // 2, HALF)
+        for s in range(3):
+            open_y(0, 1, s, s)
+        for first in (0, 2):
+            for i in (first, first + 1):
+                cast_x(vector, 1, 1, *strip(i))
+            for i in (first, first + 1):
+                quant_x(1, 1, *strip(i))
+        for i, bank in enumerate((3, 4, 6, 7)):
+            make_h(1, i, bank)
+        cast_y(vector, 0, 0)
+        cast_y(vector, 1, 0, 0, Y_CUT)
+        cast_y(scalar, 1, 0, Y_CUT, HALF)
+        quant_h(1, 0, HALF // 2)
+        quant_h(1, HALF // 2, HALF)
+        for a in range(2):
+            quant_y(a, 0)
+            store_codes(a, 0)
+        store_scales(0)
+        for s in range(3):
+            base(0, 1, s, 1)
+        for key, bank in (((0, 1, 3), 5), ((1, 1, 0), 3)):
+            open_y(*key, bank)
+            base(*key, 1)
+        for s in range(PACK):
+            branch(0, 1, s)
+            drain(vector if s % 2 else scalar, 0, 1, s)
+            if s % 2:
+                store_y(0, 1, s - 1)
+        branch(1, 1, 0)
+        drain(scalar, 1, 1, 0)
+        for s, bank in ((1, 4), (2, 6), (3, 7)):
+            open_y(1, 1, s, bank)
+            base(1, 1, s, 1)
+            branch(1, 1, s)
+        drain(scalar, 1, 1, 1)
+        store_y(1, 1, 0)
+        cast_y(vector, 0, 1)
         quant_y(0, 1)
         store_codes(0, 1)
-        interleave(nc.scalar, y_bf[1, 1], y_f32[1, 1], 3 * SUB, TC)
-        interleave(nc.vector, y_bf[1, 1], y_f32[1, 1], 0, 3 * SUB)
-        quant_y(1, 1)
+        drain(scalar, 1, 1, 2)
+        drain(scalar, 1, 1, 3, 0, HALF // 2)
+        drain(scalar, 1, 1, 3, HALF // 2, HALF)
+        store_y(1, 1, 2)
+        cast_y(vector, 1, 1, 0, HALF // 2)
+        cast_y(vector, 1, 1, *strip(2))
+        cast_y(scalar, 1, 1, *strip(3))
+        quant_y(1, 1, 0, HALF // 2)
+        quant_y(1, 1, HALF // 2, HALF)
         store_codes(1, 1)
-        store_scales(nc.scalar, 1)
+        store_scales(1)

@@ -9,6 +9,7 @@ F32 = mybir.dt.float32
 BF16 = mybir.dt.bfloat16
 I32 = mybir.dt.int32
 U32 = mybir.dt.uint32
+U16 = mybir.dt.uint16
 U8 = mybir.dt.uint8
 FP8X4 = mybir.dt.float8_e4m3fn_x4
 FP4X4 = mybir.dt.float4_e2m1fn_x4
@@ -56,8 +57,9 @@ def tile_mix_lowrank_fm_pl_none_kernel(tc, x, w4_words, w4_scales, down, up, out
         y_f32 = {ac: sbuf("y_f32%d%d" % ac, [P, PACK, HALF], F32) for ac in two_by_two}
         y_bf = {ac: sbuf("y_bf%d%d" % ac, [P, HALF, PACK], BF16) for ac in two_by_two}
         y_codes = {ac: sbuf("y_codes%d%d" % ac, [P, HALF], U32) for ac in two_by_two}
-        y_scales = [sbuf("y_scales%d" % c, [P, 2, HALF], U8) for c in range(2)]
+        y_scales = sbuf("y_scales", [P, 2, T], U8)
         y_acc = {}
+        h_acc = {}
 
         def copy(engine, out, in_):
             if engine is scalar:
@@ -106,7 +108,7 @@ def tile_mix_lowrank_fm_pl_none_kernel(tc, x, w4_words, w4_scales, down, up, out
             quantize(h_codes[c], h_scales[c], h_bf[c][:].rearrange("p t j -> p (t j)"), lo, hi)
 
         def quant_y(a, c, lo=0, hi=HALF):
-            quantize(y_codes[a, c], y_scales[c][:, a, :], y_bf[a, c][:].rearrange("p t j -> p (t j)"), lo, hi)
+            quantize(y_codes[a, c], y_scales[:, a, c * HALF:(c + 1) * HALF], y_bf[a, c][:].rearrange("p t j -> p (t j)"), lo, hi)
 
         def strip(i):
             return i * STRIP, (i + 1) * STRIP
@@ -131,142 +133,159 @@ def tile_mix_lowrank_fm_pl_none_kernel(tc, x, w4_words, w4_scales, down, up, out
                                 rhs=h_codes[c][:].bitcast(FP8X4), rhs_scale=h_scales[c][:],
                                 start=False, stop=True)
 
-        def make_h(c, i, bank):
+        def h_pass(c, i, g, bank=None):
             cols = slice(*strip(i))
-            h_acc = ps.tile([P, PACK, STRIP], F32, name="bank%d" % bank)
+            if g == 0:
+                h_acc[c, i] = ps.tile([P, PACK, STRIP], F32, name="bank%d" % bank)
+            name = "down%d" % g
             for s in range(PACK):
-                for g in range(2):
-                    name = "down%d" % g
-                    nc.tensor.matmul_mx(out=h_acc[:, s, :],
-                                        lhsT=w_codes[name][:, s * P:(s + 1) * P].bitcast(FP8X4),
-                                        lhsT_scale=w_scales[name][:, s * P:(s + 1) * P],
-                                        rhs=x_codes[g, c][:, cols].bitcast(FP8X4), rhs_scale=x_scales[g, c][:, cols],
-                                        start=(g == 0), stop=(g == 1))
-            scalar.copy(out=h_bf[c][:, cols, :], in_=h_acc[:].rearrange("p s t -> p t s"))
+                nc.tensor.matmul_mx(out=h_acc[c, i][:, s, :],
+                                    lhsT=w_codes[name][:, s * P:(s + 1) * P].bitcast(FP8X4),
+                                    lhsT_scale=w_scales[name][:, s * P:(s + 1) * P],
+                                    rhs=x_codes[g, c][:, cols].bitcast(FP8X4), rhs_scale=x_scales[g, c][:, cols],
+                                    start=(g == 0 and s == 0), stop=(g == 1 and s == PACK - 1))
+
+        def drain_h(engine, c, i):
+            copy(engine, h_bf[c][:, slice(*strip(i)), :], h_acc[c, i][:].rearrange("p s t -> p t s"))
 
         def drain(engine, a, c, s, lo=0, hi=HALF):
             copy(engine, y_f32[a, c][:, s, lo:hi], y_acc[a, c, s][:, lo:hi])
 
-        def store_y(a, c, s):
+        def store_y(a, c, s, count=2):
             rows = out_0[a * SPAN:(a + 1) * SPAN, c * HALF:(c + 1) * HALF].rearrange("(p s) t -> p s t", s=PACK)
-            nc.sync.dma_start(out=rows[:, s:s + 2, :], in_=y_f32[a, c][:, s:s + 2, :])
+            nc.sync.dma_start(out=rows[:, s:s + count, :], in_=y_f32[a, c][:, s:s + count, :])
 
         def store_codes(a, c):
             words = out_1[a].rearrange("p t j -> p (t j)").bitcast(I32)
             nc.sync.dma_start(out=words[:, c * HALF:(c + 1) * HALF], in_=y_codes[a, c][:].bitcast(I32))
 
-        def store_scales(c):
+        def store_scales():
             for quad in range(PACK):
-                rows = out_2[:, 4 * quad:4 * quad + 4, c * HALF:(c + 1) * HALF].rearrange("a q t -> q a t")
+                rows = out_2[:, 4 * quad:4 * quad + 4, :].rearrange("a q t -> q a t")
                 nc.sync.dma_start(out=rows.bitcast(I32),
-                                  in_=y_scales[c][QUAD * quad:QUAD * quad + 4, :, :].bitcast(I32))
+                                  in_=y_scales[QUAD * quad:QUAD * quad + 4, :, :].bitcast(I32))
 
-        vector.memset(s4_raw[:].rearrange("p g n -> p (g n)").bitcast(I32), 0)
-        nc.sync.dma_start(out=w4_raw[:].bitcast(I32), in_=w4_words.rearrange("g p b -> p g b").bitcast(I32))
-        for quad in range(PACK):
-            nc.sync.dma_start(out=s4_raw[QUAD * quad:QUAD * quad + 4, :, :].bitcast(I32),
-                              in_=w4_scales[:, 4 * quad:4 * quad + 4, :].rearrange("g q n -> q g n").bitcast(I32))
-        load_x(0, 0)
-        load_w("down0")
-        load_w("down1")
-        load_x(1, 0)
-        load_w("up0")
-        load_w("up1")
-        load_x(0, 1)
-        load_x(1, 1, 0, HALF // 2)
-        load_x(1, 1, HALF // 2, HALF)
+        def deal_words(a):
+            cols = slice(a * SPAN, (a + 1) * SPAN)
+            vector.tensor_copy(out=w4_dealt[:].bitcast(U16)[:, :, cols].rearrange("p g (s m) -> p g s m", s=PACK),
+                               in_=w4_raw[:].bitcast(U16)[:, :, cols].rearrange("p g (m s) -> p g s m", s=PACK))
 
-        for g, a in two_by_two:
-            cols = slice(2 * a * SPAN, 2 * (a + 1) * SPAN)
-            vector.tensor_copy(out=w4_dealt[:, g, cols].rearrange("p (s m b) -> p s m b", s=PACK, b=2),
-                               in_=w4_raw[:, g, cols].rearrange("p (m s b) -> p s m b", s=PACK, b=2))
-        for g in range(2):
+        def deal_scales(g):
             vector.tensor_copy(out=s4_dealt[:, g, :].rearrange("p (a s m) -> p a s m", a=2, s=PACK),
                                in_=s4_raw[:, g, :].rearrange("p (a m s) -> p a s m", a=2, s=PACK))
 
-        cast_x(vector, 0, 0, 0, X_CUT)
-        cast_x(scalar, 0, 0, X_CUT, HALF)
+        def load_words():
+            nc.sync.dma_start(out=w4_raw[:].bitcast(I32), in_=w4_words.rearrange("g p b -> p g b").bitcast(I32))
+
+        def load_scales():
+            for quad in range(PACK):
+                nc.sync.dma_start(out=s4_raw[QUAD * quad:QUAD * quad + 4, :, :].bitcast(I32),
+                                  in_=w4_scales[:, 4 * quad:4 * quad + 4, :].rearrange("g q n -> q g n").bitcast(I32))
+
+        vector.memset(s4_raw[:].rearrange("p g n -> p (g n)").bitcast(I32), 0)
+        load_w("down0")
+        load_scales()
+        load_w("down1")
+        load_x(0, 0)
+        load_x(1, 0)
+        load_words()
+        load_w("up0")
+        load_w("up1")
+        load_x(0, 1)
+        load_x(1, 1)
+
+        def prepare_x_by_strips(g, c):
+            cast_x(vector, g, c, *strip(0))
+            cast_x(scalar, g, c, *strip(2))
+            cast_x(vector, g, c, *strip(1))
+            quant_x(g, c, *strip(0))
+            cast_x(vector, g, c, *strip(3))
+            for i in range(1, PACK):
+                quant_x(g, c, *strip(i))
+
         cast_w_shared("down0")
+        deal_scales(0)
         quant_w("down0")
-        quant_x(0, 0)
-        early = [(0, 0, s) for s in range(PACK)] + [(1, 0, 0)]
-        for bank, key in enumerate(early):
-            open_y(*key, bank)
+        deal_scales(1)
         cast_w_shared("down1")
         quant_w("down1")
+        prepare_x_by_strips(0, 0)
         for i in range(PACK):
-            cast_x(vector if i < 2 else scalar, 1, 0, *strip(i))
+            h_pass(0, i, 0, PACK + i)
+        prepare_x_by_strips(1, 0)
         for i in range(PACK):
-            quant_x(1, 0, *strip(i))
-        for i, bank in enumerate((5, 6, 7, 5)):
-            make_h(0, i, bank)
-        cast_w(vector, "up0", 0, P)
-        quant_h(0, 0, HALF // 2)
-        quant_w("up0")
-        quant_h(0, HALF // 2, HALF)
-        cast_w_shared("up1")
-        quant_w("up1")
-        for key in early:
-            base(*key, 1)
-        open_y(1, 0, 1, 6)
-        base(1, 0, 1, 1)
+            h_pass(0, i, 1)
+            drain_h(scalar, 0, i)
+        deal_words(0)
         for s in range(PACK):
-            branch(0, 0, s)
-        for s, bank in ((2, 7), (3, 5)):
-            open_y(1, 0, s, bank)
+            open_y(0, 0, s, s)
+            base(0, 0, s, 1)
+        deal_words(1)
+        quant_h(0, 0, HALF // 2)
+        cast_w_shared("up0")
+        quant_h(0, HALF // 2, HALF)
+        quant_w("up0")
+        for s in range(2):
+            open_y(1, 0, s, PACK + s)
             base(1, 0, s, 1)
         for s in range(PACK):
+            branch(0, 0, s)
+            drain(scalar, 0, 0, s)
+        for s in range(2, PACK):
+            open_y(1, 0, s, PACK + s)
+            base(1, 0, s, 1)
+        cast_w(vector, "up1", 0, P)
+        quant_w("up1")
+        store_y(0, 0, 0, PACK)
+        cast_y(scalar, 0, 0, *strip(3))
+        for s in range(PACK):
             branch(1, 0, s)
-        drain(scalar, 0, 0, 0)
-        drain(scalar, 0, 0, 1)
-        store_y(0, 0, 0)
-        cast_x(vector, 0, 1, 0, X_CUT)
-        cast_x(scalar, 0, 1, X_CUT, HALF)
-        for a, s in ((0, 2), (1, 0), (1, 2)):
-            drain(scalar, a, 0, s)
-            drain(scalar, a, 0, s + 1)
-            store_y(a, 0, s)
+            drain(scalar, 1, 0, s)
+        store_y(1, 0, 0, PACK)
 
+        cast_x(vector, 0, 1, 0, HALF // 2)
+        cast_x(vector, 0, 1, HALF // 2, HALF)
         quant_x(0, 1, 0, HALF // 2)
         quant_x(0, 1, HALF // 2, HALF)
-        for s in range(3):
-            open_y(0, 1, s, s)
-        for first in (0, 2):
-            for i in (first, first + 1):
-                cast_x(vector, 1, 1, *strip(i))
-            for i in (first, first + 1):
-                quant_x(1, 1, *strip(i))
-        for i, bank in enumerate((3, 4, 6, 7)):
-            make_h(1, i, bank)
-        cast_y(vector, 0, 0)
-        cast_y(vector, 1, 0, 0, Y_CUT)
-        cast_y(scalar, 1, 0, Y_CUT, HALF)
-        quant_h(1, 0, HALF // 2)
-        quant_h(1, HALF // 2, HALF)
-        for a in range(2):
-            quant_y(a, 0)
-            store_codes(a, 0)
-        store_scales(0)
-        for s in range(3):
+        for i in range(PACK):
+            h_pass(1, i, 0, i)
+        cast_y(vector, 0, 0, 0, 2 * STRIP)
+        prepare_x_by_strips(1, 1)
+        cast_y(scalar, 1, 0, *strip(3))
+        open_y(0, 1, 0, PACK)
+        for i in range(PACK):
+            h_pass(1, i, 1)
+        cast_y(vector, 0, 0, *strip(2))
+        drain_h(scalar, 1, 0)
+        drain_h(scalar, 1, 1)
+        quant_y(0, 0)
+        store_codes(0, 0)
+        drain_h(vector, 1, 2)
+        drain_h(scalar, 1, 3)
+        base(0, 1, 0, 1)
+        for s in range(1, PACK):
+            open_y(0, 1, s, PACK + s)
             base(0, 1, s, 1)
-        for key, bank in (((0, 1, 3), 5), ((1, 1, 0), 3)):
-            open_y(*key, bank)
-            base(*key, 1)
+        quant_h(1, 0, HALF // 2)
+        cast_y(scalar, 1, 0, *strip(2))
+        quant_h(1, HALF // 2, HALF)
+        cast_y(vector, 1, 0, 0, 2 * STRIP)
+        quant_y(1, 0)
         for s in range(PACK):
             branch(0, 1, s)
-            drain(vector if s % 2 else scalar, 0, 1, s)
-            if s % 2:
-                store_y(0, 1, s - 1)
-        branch(1, 1, 0)
-        drain(scalar, 1, 1, 0)
-        for s, bank in ((1, 4), (2, 6), (3, 7)):
-            open_y(1, 1, s, bank)
+            drain(scalar, 0, 1, s)
+            store_y(0, 1, s, 1)
+            if s == 0:
+                store_codes(1, 0)
+        for s in range(PACK):
+            open_y(1, 1, s, s)
             base(1, 1, s, 1)
             branch(1, 1, s)
-        drain(scalar, 1, 1, 1)
-        store_y(1, 1, 0)
         cast_y(vector, 0, 1)
         quant_y(0, 1)
+        drain(scalar, 1, 1, 0)
+        drain(scalar, 1, 1, 1)
+        store_y(1, 1, 0)
         store_codes(0, 1)
         drain(scalar, 1, 1, 2)
         drain(scalar, 1, 1, 3, 0, HALF // 2)
@@ -278,4 +297,4 @@ def tile_mix_lowrank_fm_pl_none_kernel(tc, x, w4_words, w4_scales, down, up, out
         quant_y(1, 1, 0, HALF // 2)
         quant_y(1, 1, HALF // 2, HALF)
         store_codes(1, 1)
-        store_scales(1)
+        store_scales()

@@ -85,10 +85,10 @@ def tile_mix_lowrank_fm_pl_none_kernel(tc, x, w4_words, w4_scales, down, up, out
         def cast_y(engine, a, c, lo=0, hi=HALF):
             interleave(engine, y_bf[a, c], y_f32[a, c], lo, hi)
 
-        def cast_w(engine, name, lo, hi):
+        def cast_w(engine, name, lo, hi, slots=slice(0, PACK)):
             copy(engine,
-                 w_bf[name][:, :, lo:hi, :].rearrange("p s m j -> p m j s"),
-                 w_raw[name][:, :, PACK * lo:PACK * hi].rearrange("p j (m s) -> p m j s", s=PACK))
+                 w_bf[name][:, slots, lo:hi, :].rearrange("p s m j -> p m j s"),
+                 w_raw[name][:, :, PACK * lo:PACK * hi].rearrange("p j (m s) -> p m j s", s=PACK)[:, :, :, slots])
 
         def cast_w_shared(name):
             cast_w(vector, name, 0, DEAL_CUT)
@@ -101,8 +101,8 @@ def tile_mix_lowrank_fm_pl_none_kernel(tc, x, w4_words, w4_scales, down, up, out
         def quant_x(g, c, lo=0, hi=HALF):
             quantize(x_codes[g, c], x_scales[g, c], x_bf[g, c][:].rearrange("p t j -> p (t j)"), lo, hi)
 
-        def quant_w(name):
-            quantize(w_codes[name], w_scales[name], w_bf[name][:].rearrange("p s m j -> p (s m j)"), 0, SPAN)
+        def quant_w(name, lo=0, hi=SPAN):
+            quantize(w_codes[name], w_scales[name], w_bf[name][:].rearrange("p s m j -> p (s m j)"), lo, hi)
 
         def quant_h(c, lo, hi):
             quantize(h_codes[c], h_scales[c], h_bf[c][:].rearrange("p t j -> p (t j)"), lo, hi)
@@ -192,16 +192,21 @@ def tile_mix_lowrank_fm_pl_none_kernel(tc, x, w4_words, w4_scales, down, up, out
         load_w("up0")
         load_w("up1")
         load_x(0, 1)
-        load_x(1, 1)
+        load_x(1, 1, 0, HALF // 2)
+        load_x(1, 1, HALF // 2, HALF)
 
         def prepare_x_by_strips(g, c):
+            cast_x(scalar, g, c, *strip(3))
             cast_x(vector, g, c, *strip(0))
-            cast_x(scalar, g, c, *strip(2))
             cast_x(vector, g, c, *strip(1))
             quant_x(g, c, *strip(0))
-            cast_x(vector, g, c, *strip(3))
-            for i in range(1, PACK):
-                quant_x(g, c, *strip(i))
+            cast_x(vector, g, c, *strip(2))
+            quant_x(g, c, *strip(1))
+            quant_x(g, c, *strip(3))
+            quant_x(g, c, *strip(2))
+
+        first, second = slice(0, 2), slice(2, PACK)
+        strip_order = (0, 1, 3, 2)
 
         cast_w_shared("down0")
         deal_scales(0)
@@ -210,81 +215,99 @@ def tile_mix_lowrank_fm_pl_none_kernel(tc, x, w4_words, w4_scales, down, up, out
         cast_w_shared("down1")
         quant_w("down1")
         prepare_x_by_strips(0, 0)
-        for i in range(PACK):
+        for i in strip_order:
             h_pass(0, i, 0, PACK + i)
         prepare_x_by_strips(1, 0)
-        for i in range(PACK):
+        for i in strip_order:
             h_pass(0, i, 1)
-            drain_h(scalar, 0, i)
         deal_words(0)
+        deal_words(1)
+        for i in strip_order:
+            drain_h(vector if i == 2 else scalar, 0, i)
         for s in range(PACK):
             open_y(0, 0, s, s)
             base(0, 0, s, 1)
-        deal_words(1)
-        quant_h(0, 0, HALF // 2)
-        cast_w_shared("up0")
-        quant_h(0, HALF // 2, HALF)
-        quant_w("up0")
-        for s in range(2):
-            open_y(1, 0, s, PACK + s)
-            base(1, 0, s, 1)
+        cast_w(vector, "up0", 0, P, first)
+        cast_w(scalar, "up0", 0, P, second)
+        quant_h(0, 0, HALF)
+        quant_w("up0", 0, SPAN // 2)
+        quant_w("up0", SPAN // 2, SPAN)
+        open_y(1, 0, 0, PACK)
+        base(1, 0, 0, 1)
         for s in range(PACK):
             branch(0, 0, s)
             drain(scalar, 0, 0, s)
-        for s in range(2, PACK):
+            if s % 2:
+                store_y(0, 0, s - 1)
+        for s in range(1, PACK):
             open_y(1, 0, s, PACK + s)
             base(1, 0, s, 1)
-        cast_w(vector, "up1", 0, P)
-        quant_w("up1")
-        store_y(0, 0, 0, PACK)
-        cast_y(scalar, 0, 0, *strip(3))
+        cast_w(vector, "up1", 0, P, first)
+        cast_w(vector, "up1", 0, P, second)
+        quant_w("up1", 0, SPAN // 2)
+        quant_w("up1", SPAN // 2, SPAN)
         for s in range(PACK):
             branch(1, 0, s)
-            drain(scalar, 1, 0, s)
-        store_y(1, 0, 0, PACK)
 
-        cast_x(vector, 0, 1, 0, HALF // 2)
-        cast_x(vector, 0, 1, HALF // 2, HALF)
-        quant_x(0, 1, 0, HALF // 2)
-        quant_x(0, 1, HALF // 2, HALF)
-        for i in range(PACK):
+        prepare_x_by_strips(0, 1)
+        for s in range(PACK):
+            drain(scalar, 1, 0, s)
+            if s % 2:
+                store_y(1, 0, s - 1)
+        for i in strip_order:
             h_pass(1, i, 0, i)
-        cast_y(vector, 0, 0, 0, 2 * STRIP)
-        prepare_x_by_strips(1, 1)
-        cast_y(scalar, 1, 0, *strip(3))
-        open_y(0, 1, 0, PACK)
-        for i in range(PACK):
-            h_pass(1, i, 1)
-        cast_y(vector, 0, 0, *strip(2))
+        for s in range(2):
+            open_y(0, 1, s, PACK + s)
+        cast_x(vector, 1, 1, *strip(0))
+        cast_x(vector, 1, 1, *strip(1))
+        quant_x(1, 1, *strip(0))
+        cast_x(vector, 1, 1, *strip(2))
+        cast_x(scalar, 1, 1, *strip(3))
+        quant_x(1, 1, *strip(1))
+        quant_x(1, 1, *strip(2))
+        quant_x(1, 1, *strip(3))
+        h_pass(1, 0, 1)
+        h_pass(1, 1, 1)
+        open_y(0, 1, 2, PACK + 2)
+        h_pass(1, 2, 1)
+        h_pass(1, 3, 1)
+        open_y(0, 1, 3, PACK + 3)
+        for s in range(PACK):
+            base(0, 1, s, 1)
+        cast_y(vector, 0, 0)
         drain_h(scalar, 1, 0)
         drain_h(scalar, 1, 1)
+        drain_h(scalar, 1, 2)
+        drain_h(vector, 1, 3)
+        quant_h(1, 0, HALF // 2)
+        quant_h(1, *strip(2))
+        quant_h(1, *strip(3))
         quant_y(0, 0)
         store_codes(0, 0)
-        drain_h(vector, 1, 2)
-        drain_h(scalar, 1, 3)
-        base(0, 1, 0, 1)
-        for s in range(1, PACK):
-            open_y(0, 1, s, PACK + s)
-            base(0, 1, s, 1)
-        quant_h(1, 0, HALF // 2)
-        cast_y(scalar, 1, 0, *strip(2))
-        quant_h(1, HALF // 2, HALF)
-        cast_y(vector, 1, 0, 0, 2 * STRIP)
-        quant_y(1, 0)
+        cast_y(scalar, 1, 0, HALF // 2, HALF)
+        cast_y(vector, 1, 0, 0, HALF // 2)
+        open_y(1, 1, 0, 0)
+        base(1, 1, 0, 1)
         for s in range(PACK):
             branch(0, 1, s)
-            drain(scalar, 0, 1, s)
+        drain(scalar, 0, 1, 0)
+        quant_y(1, 0)
+        store_y(0, 1, 0, 1)
+        store_codes(1, 0)
+        drain(vector, 0, 1, 1)
+        drain(scalar, 0, 1, 2)
+        drain(vector, 0, 1, 3)
+        for s in range(1, PACK):
             store_y(0, 1, s, 1)
-            if s == 0:
-                store_codes(1, 0)
-        for s in range(PACK):
+        branch(1, 1, 0)
+        for s in range(1, PACK):
             open_y(1, 1, s, s)
             base(1, 1, s, 1)
             branch(1, 1, s)
         cast_y(vector, 0, 1)
-        quant_y(0, 1)
         drain(scalar, 1, 1, 0)
         drain(scalar, 1, 1, 1)
+        quant_y(0, 1)
         store_y(1, 1, 0)
         store_codes(0, 1)
         drain(scalar, 1, 1, 2)

@@ -57,7 +57,7 @@ def tile_mix_lowrank_fm_pl_none_kernel(tc, x, w4_words, w4_scales, down, up, out
         y_f32 = {ac: sbuf("y_f32%d%d" % ac, [P, PACK, HALF], F32) for ac in two_by_two}
         y_bf = {ac: sbuf("y_bf%d%d" % ac, [P, HALF, PACK], BF16) for ac in two_by_two}
         y_codes = {ac: sbuf("y_codes%d%d" % ac, [P, HALF], U32) for ac in two_by_two}
-        y_scales = sbuf("y_scales", [P, 2, T], U8)
+        y_scales = [sbuf("y_scales%d" % c, [P, 2, HALF], U8) for c in range(2)]
         y_acc = {}
         h_acc = {}
 
@@ -108,7 +108,7 @@ def tile_mix_lowrank_fm_pl_none_kernel(tc, x, w4_words, w4_scales, down, up, out
             quantize(h_codes[c], h_scales[c], h_bf[c][:].rearrange("p t j -> p (t j)"), lo, hi)
 
         def quant_y(a, c, lo=0, hi=HALF):
-            quantize(y_codes[a, c], y_scales[:, a, c * HALF:(c + 1) * HALF], y_bf[a, c][:].rearrange("p t j -> p (t j)"), lo, hi)
+            quantize(y_codes[a, c], y_scales[c][:, a, :], y_bf[a, c][:].rearrange("p t j -> p (t j)"), lo, hi)
 
         def strip(i):
             return i * STRIP, (i + 1) * STRIP
@@ -159,11 +159,11 @@ def tile_mix_lowrank_fm_pl_none_kernel(tc, x, w4_words, w4_scales, down, up, out
             words = out_1[a].rearrange("p t j -> p (t j)").bitcast(I32)
             nc.sync.dma_start(out=words[:, c * HALF:(c + 1) * HALF], in_=y_codes[a, c][:].bitcast(I32))
 
-        def store_scales():
+        def store_scales(c):
             for quad in range(PACK):
-                rows = out_2[:, 4 * quad:4 * quad + 4, :].rearrange("a q t -> q a t")
+                rows = out_2[:, 4 * quad:4 * quad + 4, c * HALF:(c + 1) * HALF].rearrange("a q t -> q a t")
                 nc.sync.dma_start(out=rows.bitcast(I32),
-                                  in_=y_scales[QUAD * quad:QUAD * quad + 4, :, :].bitcast(I32))
+                                  in_=y_scales[c][QUAD * quad:QUAD * quad + 4, :, :].bitcast(I32))
 
         def deal_words(a):
             cols = slice(a * SPAN, (a + 1) * SPAN)
@@ -294,6 +294,7 @@ def tile_mix_lowrank_fm_pl_none_kernel(tc, x, w4_words, w4_scales, down, up, out
         quant_y(1, 0)
         store_y(0, 1, 0, 1)
         store_codes(1, 0)
+        store_scales(0)
         drain(vector, 0, 1, 1)
         drain(scalar, 0, 1, 2)
         drain(vector, 0, 1, 3)
@@ -313,11 +314,12 @@ def tile_mix_lowrank_fm_pl_none_kernel(tc, x, w4_words, w4_scales, down, up, out
         drain(scalar, 1, 1, 2)
         drain(scalar, 1, 1, 3, 0, HALF // 2)
         drain(scalar, 1, 1, 3, HALF // 2, HALF)
-        store_y(1, 1, 2)
+        store_y(1, 1, 2, 1)
         cast_y(vector, 1, 1, 0, HALF // 2)
         cast_y(vector, 1, 1, *strip(2))
         cast_y(scalar, 1, 1, *strip(3))
         quant_y(1, 1, 0, HALF // 2)
         quant_y(1, 1, HALF // 2, HALF)
+        store_scales(1)
         store_codes(1, 1)
-        store_scales()
+        store_y(1, 1, 3, 1)

@@ -23,7 +23,8 @@ QUAD = 32
 
 DEAL_CUT = 80
 X_CUT = 384
-Y_CUT = 320
+Y0_CUT = 128
+Y_CUT = 384
 
 
 def tile_mix_lowrank_fm_pl_none_kernel(tc, x, w4_words, w4_scales, down, up, out_0, out_1, out_2):
@@ -183,12 +184,12 @@ def tile_mix_lowrank_fm_pl_none_kernel(tc, x, w4_words, w4_scales, down, up, out
                                   in_=w4_scales[:, 4 * quad:4 * quad + 4, :].rearrange("g q n -> q g n").bitcast(I32))
 
         vector.memset(s4_raw[:].rearrange("p g n -> p (g n)").bitcast(I32), 0)
-        load_w("down0")
-        load_scales()
-        load_w("down1")
-        load_x(0, 0)
-        load_x(1, 0)
         load_words()
+        load_scales()
+        load_w("down0")
+        load_x(0, 0)
+        load_w("down1")
+        load_x(1, 0)
         load_w("up0")
         load_w("up1")
         load_x(0, 1)
@@ -208,73 +209,79 @@ def tile_mix_lowrank_fm_pl_none_kernel(tc, x, w4_words, w4_scales, down, up, out
         first, second = slice(0, 2), slice(2, PACK)
         strip_order = (0, 1, 3, 2)
 
+        for a in range(2):
+            deal_words(a)
+        for g in range(2):
+            deal_scales(g)
         cast_w_shared("down0")
-        deal_scales(0)
         quant_w("down0")
-        deal_scales(1)
+        prepare_x_by_strips(0, 0)
         cast_w_shared("down1")
         quant_w("down1")
-        prepare_x_by_strips(0, 0)
+        for s in range(PACK):
+            open_y(0, 0, s, s)
         for i in strip_order:
             h_pass(0, i, 0, PACK + i)
         prepare_x_by_strips(1, 0)
         for i in strip_order:
             h_pass(0, i, 1)
-        deal_words(0)
-        deal_words(1)
-        for i in strip_order:
-            drain_h(vector if i == 2 else scalar, 0, i)
         for s in range(PACK):
-            open_y(0, 0, s, s)
             base(0, 0, s, 1)
+        drain_h(scalar, 0, 0)
+        drain_h(scalar, 0, 1)
         cast_w(vector, "up0", 0, P, first)
+        drain_h(vector, 0, 2)
+        drain_h(scalar, 0, 3)
         cast_w(scalar, "up0", 0, P, second)
-        quant_h(0, 0, HALF)
         quant_w("up0", 0, SPAN // 2)
-        quant_w("up0", SPAN // 2, SPAN)
-        open_y(1, 0, 0, PACK)
-        base(1, 0, 0, 1)
-        for s in range(PACK):
-            branch(0, 0, s)
-            drain(scalar, 0, 0, s)
-            if s % 2:
-                store_y(0, 0, s - 1)
-        for s in range(1, PACK):
+        quant_h(0, 0, HALF)
+        for s in range(2):
             open_y(1, 0, s, PACK + s)
             base(1, 0, s, 1)
+        open_y(1, 0, 3, PACK + 3)
+        quant_w("up0", SPAN // 2, SPAN)
+        for s in range(PACK):
+            branch(0, 0, s)
+            if s == 1:
+                base(1, 0, 3, 1)
+        open_y(1, 0, 2, PACK + 2)
+        base(1, 0, 2, 1)
         cast_w(vector, "up1", 0, P, first)
         cast_w(vector, "up1", 0, P, second)
         quant_w("up1", 0, SPAN // 2)
         quant_w("up1", SPAN // 2, SPAN)
         for s in range(PACK):
-            branch(1, 0, s)
-
-        prepare_x_by_strips(0, 1)
+            drain(vector if s == 3 else scalar, 0, 0, s)
+            if s % 2:
+                store_y(0, 0, s - 1)
         for s in range(PACK):
+            branch(1, 0, s)
             drain(scalar, 1, 0, s)
             if s % 2:
                 store_y(1, 0, s - 1)
-        for i in strip_order:
+
+        cast_x(vector, 0, 1, 0, HALF // 2)
+        cast_x(vector, 0, 1, HALF // 2, HALF)
+        quant_x(0, 1, 0, HALF // 2)
+        quant_x(0, 1, HALF // 2, HALF)
+        for i in range(PACK):
             h_pass(1, i, 0, i)
-        for s in range(2):
-            open_y(0, 1, s, PACK + s)
-        cast_x(vector, 1, 1, *strip(0))
-        cast_x(vector, 1, 1, *strip(1))
-        quant_x(1, 1, *strip(0))
+        open_y(0, 1, 0, PACK)
+        cast_x(vector, 1, 1, 0, HALF // 2)
+        cast_y(vector, 0, 0, 0, Y0_CUT)
+        quant_x(1, 1, 0, HALF // 2)
         cast_x(vector, 1, 1, *strip(2))
-        cast_x(scalar, 1, 1, *strip(3))
-        quant_x(1, 1, *strip(1))
+        cast_x(vector, 1, 1, *strip(3))
         quant_x(1, 1, *strip(2))
         quant_x(1, 1, *strip(3))
-        h_pass(1, 0, 1)
-        h_pass(1, 1, 1)
-        open_y(0, 1, 2, PACK + 2)
-        h_pass(1, 2, 1)
-        h_pass(1, 3, 1)
-        open_y(0, 1, 3, PACK + 3)
+        for i in range(PACK):
+            h_pass(1, i, 1)
+        for s in range(1, PACK):
+            open_y(0, 1, s, PACK + s)
         for s in range(PACK):
             base(0, 1, s, 1)
-        cast_y(vector, 0, 0)
+        cast_y(scalar, 0, 0, Y0_CUT, HALF)
+        cast_y(vector, 1, 0, 0, Y_CUT)
         drain_h(scalar, 1, 0)
         drain_h(scalar, 1, 1)
         drain_h(scalar, 1, 2)
@@ -282,24 +289,17 @@ def tile_mix_lowrank_fm_pl_none_kernel(tc, x, w4_words, w4_scales, down, up, out
         quant_h(1, 0, HALF // 2)
         quant_h(1, *strip(2))
         quant_h(1, *strip(3))
-        quant_y(0, 0)
-        store_codes(0, 0)
-        cast_y(scalar, 1, 0, HALF // 2, HALF)
-        cast_y(vector, 1, 0, 0, HALF // 2)
-        open_y(1, 1, 0, 0)
-        base(1, 1, 0, 1)
+        cast_y(scalar, 1, 0, Y_CUT, HALF)
+        for a in range(2):
+            quant_y(a, 0)
+            store_codes(a, 0)
         for s in range(PACK):
             branch(0, 1, s)
-        drain(scalar, 0, 1, 0)
-        quant_y(1, 0)
-        store_y(0, 1, 0, 1)
-        store_codes(1, 0)
-        store_scales(0)
-        drain(vector, 0, 1, 1)
-        drain(scalar, 0, 1, 2)
-        drain(vector, 0, 1, 3)
-        for s in range(1, PACK):
+            drain(vector if s % 2 else scalar, 0, 1, s)
             store_y(0, 1, s, 1)
+        store_scales(0)
+        open_y(1, 1, 0, 0)
+        base(1, 1, 0, 1)
         branch(1, 1, 0)
         for s in range(1, PACK):
             open_y(1, 1, s, s)
@@ -314,12 +314,11 @@ def tile_mix_lowrank_fm_pl_none_kernel(tc, x, w4_words, w4_scales, down, up, out
         drain(scalar, 1, 1, 2)
         drain(scalar, 1, 1, 3, 0, HALF // 2)
         drain(scalar, 1, 1, 3, HALF // 2, HALF)
-        store_y(1, 1, 2, 1)
+        store_y(1, 1, 2)
         cast_y(vector, 1, 1, 0, HALF // 2)
         cast_y(vector, 1, 1, *strip(2))
         cast_y(scalar, 1, 1, *strip(3))
         quant_y(1, 1, 0, HALF // 2)
         quant_y(1, 1, HALF // 2, HALF)
-        store_scales(1)
         store_codes(1, 1)
-        store_y(1, 1, 3, 1)
+        store_scales(1)

@@ -36,7 +36,7 @@ def tile_mix_lowrank_fm_pl_none_kernel(tc, x, w4_words, w4_scales, down, up, out
         ctx.enter_context(tc.manual_schedule())
 
         def sbuf(name, shape, dtype):
-            return sb.tile(shape, dtype, name=name, align_bytes=64)
+            return sb.tile(shape, dtype, name=name, align_bytes=256)
 
         two_by_two = [(i, j) for i in range(2) for j in range(2)]
         x_raw = {gc: sbuf("x_raw%d%d" % gc, [P, PACK, HALF], F32) for gc in two_by_two}

@@ -23,8 +23,9 @@ QUAD = 32
 
 DEAL_CUT = 80
 X_CUT = 384
+UP_CUT = 32
 Y0_CUT = 128
-Y_CUT = 384
+Y_CUT = 256
 
 
 def tile_mix_lowrank_fm_pl_none_kernel(tc, x, w4_words, w4_scales, down, up, out_0, out_1, out_2):
@@ -228,10 +229,10 @@ def tile_mix_lowrank_fm_pl_none_kernel(tc, x, w4_words, w4_scales, down, up, out
         for s in range(PACK):
             base(0, 0, s, 1)
         drain_h(scalar, 0, 0)
-        drain_h(scalar, 0, 1)
+        drain_h(vector, 0, 1)
+        drain_h(scalar, 0, 3)
         cast_w(vector, "up0", 0, P, first)
         drain_h(vector, 0, 2)
-        drain_h(scalar, 0, 3)
         cast_w(scalar, "up0", 0, P, second)
         quant_w("up0", 0, SPAN // 2)
         quant_h(0, 0, HALF)
@@ -240,6 +241,7 @@ def tile_mix_lowrank_fm_pl_none_kernel(tc, x, w4_words, w4_scales, down, up, out
             base(1, 0, s, 1)
         open_y(1, 0, 3, PACK + 3)
         quant_w("up0", SPAN // 2, SPAN)
+        cast_w(scalar, "up1", UP_CUT, P, second)
         for s in range(PACK):
             branch(0, 0, s)
             if s == 1:
@@ -247,11 +249,11 @@ def tile_mix_lowrank_fm_pl_none_kernel(tc, x, w4_words, w4_scales, down, up, out
         open_y(1, 0, 2, PACK + 2)
         base(1, 0, 2, 1)
         cast_w(vector, "up1", 0, P, first)
-        cast_w(vector, "up1", 0, P, second)
+        cast_w(vector, "up1", 0, UP_CUT, second)
         quant_w("up1", 0, SPAN // 2)
         quant_w("up1", SPAN // 2, SPAN)
         for s in range(PACK):
-            drain(vector if s == 3 else scalar, 0, 0, s)
+            drain(scalar, 0, 0, s)
             if s % 2:
                 store_y(0, 0, s - 1)
         for s in range(PACK):
@@ -260,43 +262,39 @@ def tile_mix_lowrank_fm_pl_none_kernel(tc, x, w4_words, w4_scales, down, up, out
             if s % 2:
                 store_y(1, 0, s - 1)
 
-        cast_x(vector, 0, 1, 0, HALF // 2)
-        cast_x(vector, 0, 1, HALF // 2, HALF)
-        quant_x(0, 1, 0, HALF // 2)
-        quant_x(0, 1, HALF // 2, HALF)
+        for g in range(2):
+            for lo in (0, HALF // 2):
+                cast_x(vector, g, 1, lo, lo + HALF // 2)
+            for lo in (0, HALF // 2):
+                quant_x(g, 1, lo, lo + HALF // 2)
         for i in range(PACK):
             h_pass(1, i, 0, i)
-        open_y(0, 1, 0, PACK)
-        cast_x(vector, 1, 1, 0, HALF // 2)
-        cast_y(vector, 0, 0, 0, Y0_CUT)
-        quant_x(1, 1, 0, HALF // 2)
-        cast_x(vector, 1, 1, *strip(2))
-        cast_x(vector, 1, 1, *strip(3))
-        quant_x(1, 1, *strip(2))
-        quant_x(1, 1, *strip(3))
+        for s in range(2):
+            open_y(0, 1, s, PACK + s)
         for i in range(PACK):
             h_pass(1, i, 1)
-        for s in range(1, PACK):
+        for s in range(2, PACK):
             open_y(0, 1, s, PACK + s)
         for s in range(PACK):
             base(0, 1, s, 1)
-        cast_y(scalar, 0, 0, Y0_CUT, HALF)
-        cast_y(vector, 1, 0, 0, Y_CUT)
-        drain_h(scalar, 1, 0)
-        drain_h(scalar, 1, 1)
-        drain_h(scalar, 1, 2)
-        drain_h(vector, 1, 3)
+        cast_y(scalar, 0, 0, 3 * STRIP, HALF)
+        cast_y(vector, 0, 0, 0, 3 * STRIP)
+        for i in range(PACK):
+            drain_h(vector if i % 2 else scalar, 1, i)
         quant_h(1, 0, HALF // 2)
-        quant_h(1, *strip(2))
-        quant_h(1, *strip(3))
+        quant_h(1, HALF // 2, HALF)
+        quant_y(0, 0)
+        store_codes(0, 0)
         cast_y(scalar, 1, 0, Y_CUT, HALF)
-        for a in range(2):
-            quant_y(a, 0)
-            store_codes(a, 0)
+        cast_y(vector, 1, 0, 0, Y_CUT)
+        quant_y(1, 0, Y_CUT, HALF)
+        quant_y(1, 0, 0, Y_CUT)
         for s in range(PACK):
             branch(0, 1, s)
-            drain(vector if s % 2 else scalar, 0, 1, s)
+            drain(vector if s == 3 else scalar, 0, 1, s)
             store_y(0, 1, s, 1)
+            if s == 0:
+                store_codes(1, 0)
         store_scales(0)
         open_y(1, 1, 0, 0)
         base(1, 1, 0, 1)

@@ -24,7 +24,6 @@ QUAD = 32
 DEAL_CUT = 80
 X_CUT = 384
 UP_CUT = 32
-Y0_CUT = 128
 Y_CUT = 256
 
 
@@ -258,42 +257,52 @@ def tile_mix_lowrank_fm_pl_none_kernel(tc, x, w4_words, w4_scales, down, up, out
                 store_y(0, 0, s - 1)
         for s in range(PACK):
             branch(1, 0, s)
+        for s in range(PACK):
+            if s == 2:
+                cast_x(scalar, 1, 1, *strip(3))
             drain(scalar, 1, 0, s)
             if s % 2:
                 store_y(1, 0, s - 1)
 
-        for g in range(2):
-            for lo in (0, HALF // 2):
-                cast_x(vector, g, 1, lo, lo + HALF // 2)
-            for lo in (0, HALF // 2):
-                quant_x(g, 1, lo, lo + HALF // 2)
+        for lo in (0, HALF // 2):
+            cast_x(vector, 0, 1, lo, lo + HALF // 2)
+        for lo in (0, HALF // 2):
+            quant_x(0, 1, lo, lo + HALF // 2)
+        cast_x(vector, 1, 1, 0, HALF // 2)
+        cast_x(vector, 1, 1, *strip(2))
+        quant_x(1, 1, 0, HALF // 2)
+        quant_x(1, 1, *strip(2))
+        quant_x(1, 1, *strip(3))
         for i in range(PACK):
             h_pass(1, i, 0, i)
-        for s in range(2):
-            open_y(0, 1, s, PACK + s)
+        open_y(0, 1, 0, PACK)
         for i in range(PACK):
             h_pass(1, i, 1)
-        for s in range(2, PACK):
+        base(0, 1, 0, 1)
+        for s in range(1, 3):
             open_y(0, 1, s, PACK + s)
-        for s in range(PACK):
             base(0, 1, s, 1)
-        cast_y(scalar, 0, 0, 3 * STRIP, HALF)
+        open_y(0, 1, 3, PACK + 3)
         cast_y(vector, 0, 0, 0, 3 * STRIP)
         for i in range(PACK):
             drain_h(vector if i % 2 else scalar, 1, i)
+        cast_y(scalar, 0, 0, 3 * STRIP, HALF)
         quant_h(1, 0, HALF // 2)
         quant_h(1, HALF // 2, HALF)
         quant_y(0, 0)
         store_codes(0, 0)
         cast_y(scalar, 1, 0, Y_CUT, HALF)
+        for s in range(PACK):
+            if s == 1:
+                base(0, 1, 3, 1)
+            branch(0, 1, s)
+            drain(scalar if s else vector, 0, 1, s)
         cast_y(vector, 1, 0, 0, Y_CUT)
         quant_y(1, 0, Y_CUT, HALF)
         quant_y(1, 0, 0, Y_CUT)
         for s in range(PACK):
-            branch(0, 1, s)
-            drain(vector if s == 3 else scalar, 0, 1, s)
             store_y(0, 1, s, 1)
-            if s == 0:
+            if s == 2:
                 store_codes(1, 0)
         store_scales(0)
         open_y(1, 1, 0, 0)

@@ -44,7 +44,7 @@ def tile_mix_lowrank_fm_pl_none_kernel(tc, x, w4_words, w4_scales, down, up, out
         x_codes = {gc: sbuf("x_codes%d%d" % gc, [P, HALF], U32) for gc in two_by_two}
         x_scales = {gc: sbuf("x_scales%d%d" % gc, [P, HALF], U8) for gc in two_by_two}
         pieces = {"down0": down[:SPAN, :], "down1": down[SPAN:, :], "up0": up[:, :SPAN], "up1": up[:, SPAN:]}
-        w_raw = {name: sbuf(name + "_raw", [P, PACK, SPAN], F32) for name in pieces}
+        w_raw = {name: sbuf(name + "_raw", [P, PACK, SPAN + 64], F32)[:, :, :SPAN] for name in pieces}
         w_bf = {name: sbuf(name + "_bf", [P, PACK, P, PACK], BF16) for name in pieces}
         w_codes = {name: sbuf(name + "_codes", [P, SPAN], U32) for name in pieces}
         w_scales = {name: sbuf(name + "_scales", [P, SPAN], U8) for name in pieces}
@@ -73,7 +73,7 @@ def tile_mix_lowrank_fm_pl_none_kernel(tc, x, w4_words, w4_scales, down, up, out
             nc.sync.dma_start(out=x_raw[g, c][:, :, lo:hi], in_=rows.rearrange("(p j) t -> p j t", j=PACK))
 
         def load_w(name):
-            nc.sync.dma_start(out=w_raw[name][:], in_=pieces[name].rearrange("(p j) n -> p j n", j=PACK))
+            nc.sync.dma_start(out=w_raw[name], in_=pieces[name].rearrange("(p j) n -> p j n", j=PACK))
 
         def interleave(engine, dst, src, lo, hi):
             copy(engine,

@@ -39,12 +39,12 @@ def tile_mix_lowrank_fm_pl_none_kernel(tc, x, w4_words, w4_scales, down, up, out
             return sb.tile(shape, dtype, name=name, align_bytes=256)
 
         two_by_two = [(i, j) for i in range(2) for j in range(2)]
-        x_raw = {gc: sbuf("x_raw%d%d" % gc, [P, PACK, HALF], F32) for gc in two_by_two}
+        x_raw = {}
         x_bf = {gc: sbuf("x_bf%d%d" % gc, [P, HALF, PACK], BF16) for gc in two_by_two}
         x_codes = {gc: sbuf("x_codes%d%d" % gc, [P, HALF], U32) for gc in two_by_two}
         x_scales = {gc: sbuf("x_scales%d%d" % gc, [P, HALF], U8) for gc in two_by_two}
         pieces = {"down0": down[:SPAN, :], "down1": down[SPAN:, :], "up0": up[:, :SPAN], "up1": up[:, SPAN:]}
-        w_raw = {name: sbuf(name + "_raw", [P, PACK, SPAN + 64], F32)[:, :, :SPAN] for name in pieces}
+        w_raw = {}
         w_bf = {name: sbuf(name + "_bf", [P, PACK, P, PACK], BF16) for name in pieces}
         w_codes = {name: sbuf(name + "_codes", [P, SPAN], U32) for name in pieces}
         w_scales = {name: sbuf(name + "_scales", [P, SPAN], U8) for name in pieces}
@@ -70,26 +70,30 @@ def tile_mix_lowrank_fm_pl_none_kernel(tc, x, w4_words, w4_scales, down, up, out
 
         def load_x(g, c, lo=0, hi=HALF):
             rows = x[g * SPAN:(g + 1) * SPAN, c * HALF + lo:c * HALF + hi]
-            nc.sync.dma_start(out=x_raw[g, c][:, :, lo:hi], in_=rows.rearrange("(p j) t -> p j t", j=PACK))
+            x_raw[g, c, lo] = sbuf("x_raw%d%d_%d" % (g, c, lo), [P, PACK, hi - lo], F32)
+            nc.sync.dma_start(out=x_raw[g, c, lo][:], in_=rows.rearrange("(p j) t -> p j t", j=PACK))
 
-        def load_w(name):
-            nc.sync.dma_start(out=w_raw[name], in_=pieces[name].rearrange("(p j) n -> p j n", j=PACK))
+        def load_w(name, lo=0, hi=SPAN):
+            w_raw[name, lo] = sbuf("%s_raw%d" % (name, lo), [P, PACK, hi - lo], F32)
+            nc.sync.dma_start(out=w_raw[name, lo][:],
+                              in_=pieces[name][:, lo:hi].rearrange("(p j) n -> p j n", j=PACK))
 
-        def interleave(engine, dst, src, lo, hi):
-            copy(engine,
-                 dst[:, lo:hi, :].rearrange("p (u i) j -> p u j i", i=4),
-                 src[:, :, lo:hi].rearrange("p j (u i) -> p u j i", i=4))
+        def interleave(engine, dst, src):
+            copy(engine, dst.rearrange("p (u i) j -> p u j i", i=4), src.rearrange("p j (u i) -> p u j i", i=4))
 
         def cast_x(engine, g, c, lo, hi):
-            interleave(engine, x_bf[g, c], x_raw[g, c], lo, hi)
+            at = max(key[2] for key in x_raw if key[:2] == (g, c) and key[2] <= lo)
+            interleave(engine, x_bf[g, c][:, lo:hi, :], x_raw[g, c, at][:, :, lo - at:hi - at])
 
         def cast_y(engine, a, c, lo=0, hi=HALF):
-            interleave(engine, y_bf[a, c], y_f32[a, c], lo, hi)
+            interleave(engine, y_bf[a, c][:, lo:hi, :], y_f32[a, c][:, :, lo:hi])
 
         def cast_w(engine, name, lo, hi, slots=slice(0, PACK)):
+            at = max(key[1] for key in w_raw if key[0] == name and key[1] <= PACK * lo)
+            raw = w_raw[name, at][:, :, PACK * lo - at:PACK * hi - at]
             copy(engine,
                  w_bf[name][:, slots, lo:hi, :].rearrange("p s m j -> p m j s"),
-                 w_raw[name][:, :, PACK * lo:PACK * hi].rearrange("p j (m s) -> p m j s", s=PACK)[:, :, :, slots])
+                 raw.rearrange("p j (m s) -> p m j s", s=PACK)[:, :, :, slots])
 
         def cast_w_shared(name):
             cast_w(vector, name, 0, DEAL_CUT)
@@ -184,71 +188,77 @@ def tile_mix_lowrank_fm_pl_none_kernel(tc, x, w4_words, w4_scales, down, up, out
                                   in_=w4_scales[:, 4 * quad:4 * quad + 4, :].rearrange("g q n -> q g n").bitcast(I32))
 
         vector.memset(s4_raw[:].rearrange("p g n -> p (g n)").bitcast(I32), 0)
+        parts = ((0, HALF // 2), (HALF // 2, HALF))
+        first, second = slice(0, 2), slice(2, PACK)
         load_words()
         load_scales()
-        load_w("down0")
         load_x(0, 0)
+        load_w("down0")
         load_w("down1")
-        load_x(1, 0)
-        load_w("up0")
-        load_w("up1")
-        load_x(0, 1)
-        load_x(1, 1, 0, HALF // 2)
-        load_x(1, 1, HALF // 2, HALF)
-
-        def prepare_x_by_strips(g, c):
-            cast_x(scalar, g, c, *strip(3))
-            cast_x(vector, g, c, *strip(0))
-            cast_x(vector, g, c, *strip(1))
-            quant_x(g, c, *strip(0))
-            cast_x(vector, g, c, *strip(2))
-            quant_x(g, c, *strip(1))
-            quant_x(g, c, *strip(3))
-            quant_x(g, c, *strip(2))
-
-        first, second = slice(0, 2), slice(2, PACK)
-        strip_order = (0, 1, 3, 2)
+        for part in parts:
+            load_x(1, 0, *part)
+        for name in ("up0", "up1"):
+            for part in parts:
+                load_w(name, *part)
+        for g in range(2):
+            for part in parts:
+                load_x(g, 1, *part)
 
         for a in range(2):
             deal_words(a)
         for g in range(2):
             deal_scales(g)
-        cast_w_shared("down0")
-        quant_w("down0")
-        prepare_x_by_strips(0, 0)
-        cast_w_shared("down1")
-        quant_w("down1")
+        cast_x(scalar, 0, 0, *strip(3))
+        cast_x(vector, 0, 0, *parts[0])
+        cast_x(vector, 0, 0, *strip(2))
+        quant_x(0, 0, *parts[0])
+        quant_x(0, 0, *parts[1])
         for s in range(PACK):
             open_y(0, 0, s, s)
-        for i in strip_order:
-            h_pass(0, i, 0, PACK + i)
-        prepare_x_by_strips(1, 0)
-        for i in strip_order:
+        for name in ("down0", "down1"):
+            cast_w(scalar, name, 0, P, slice(3, PACK))
+            cast_w(vector, name, 0, P, first)
+            cast_w(vector, name, 0, P, slice(2, 3))
+            quant_w(name, 0, SPAN // 2)
+            quant_w(name, SPAN // 2, SPAN)
+            if name == "down0":
+                for i in range(PACK):
+                    h_pass(0, i, 0, PACK + i)
+        cast_x(scalar, 1, 0, *strip(0))
+        cast_x(vector, 1, 0, *strip(1))
+        quant_x(1, 0, *strip(0))
+        cast_x(scalar, 1, 0, *strip(3))
+        cast_x(vector, 1, 0, *strip(2))
+        quant_x(1, 0, *strip(1))
+        quant_x(1, 0, *strip(2))
+        quant_x(1, 0, *strip(3))
+        for i in range(PACK):
             h_pass(0, i, 1)
         for s in range(PACK):
             base(0, 0, s, 1)
         drain_h(scalar, 0, 0)
-        drain_h(vector, 0, 1)
-        drain_h(scalar, 0, 3)
-        cast_w(vector, "up0", 0, P, first)
+        drain_h(scalar, 0, 1)
+        cast_w(vector, "up0", 0, P // 2)
         drain_h(vector, 0, 2)
-        cast_w(scalar, "up0", 0, P, second)
+        drain_h(vector, 0, 3)
+        cast_w(scalar, "up0", P // 2, P, first)
+        cast_w(scalar, "up0", P // 2, P, second)
+        quant_h(0, 0, HALF // 2)
+        quant_h(0, HALF // 2, HALF)
         quant_w("up0", 0, SPAN // 2)
-        quant_h(0, 0, HALF)
+        quant_w("up0", SPAN // 2, SPAN)
         for s in range(2):
             open_y(1, 0, s, PACK + s)
             base(1, 0, s, 1)
-        open_y(1, 0, 3, PACK + 3)
-        quant_w("up0", SPAN // 2, SPAN)
-        cast_w(scalar, "up1", UP_CUT, P, second)
+        cast_w(scalar, "up1", 0, P // 2, first)
+        cast_w(vector, "up1", 0, P // 2, second)
         for s in range(PACK):
             branch(0, 0, s)
-            if s == 1:
-                base(1, 0, 3, 1)
-        open_y(1, 0, 2, PACK + 2)
-        base(1, 0, 2, 1)
-        cast_w(vector, "up1", 0, P, first)
-        cast_w(vector, "up1", 0, UP_CUT, second)
+        for s in range(2, PACK):
+            open_y(1, 0, s, PACK + s)
+            base(1, 0, s, 1)
+        cast_w(vector, "up1", P // 2, P, first)
+        cast_w(vector, "up1", P // 2, P, second)
         quant_w("up1", 0, SPAN // 2)
         quant_w("up1", SPAN // 2, SPAN)
         for s in range(PACK):
@@ -258,64 +268,64 @@ def tile_mix_lowrank_fm_pl_none_kernel(tc, x, w4_words, w4_scales, down, up, out
         for s in range(PACK):
             branch(1, 0, s)
         for s in range(PACK):
-            if s == 2:
-                cast_x(scalar, 1, 1, *strip(3))
             drain(scalar, 1, 0, s)
             if s % 2:
                 store_y(1, 0, s - 1)
 
-        for lo in (0, HALF // 2):
-            cast_x(vector, 0, 1, lo, lo + HALF // 2)
-        for lo in (0, HALF // 2):
-            quant_x(0, 1, lo, lo + HALF // 2)
-        cast_x(vector, 1, 1, 0, HALF // 2)
-        cast_x(vector, 1, 1, *strip(2))
-        quant_x(1, 1, 0, HALF // 2)
-        quant_x(1, 1, *strip(2))
-        quant_x(1, 1, *strip(3))
+        for g in range(2):
+            for pair in ((0, 1), (2, 3)):
+                for i in pair:
+                    cast_x(vector, g, 1, *strip(i))
+                for i in pair:
+                    quant_x(g, 1, *strip(i))
         for i in range(PACK):
             h_pass(1, i, 0, i)
         open_y(0, 1, 0, PACK)
-        for i in range(PACK):
+        for i in range(2):
             h_pass(1, i, 1)
-        base(0, 1, 0, 1)
-        for s in range(1, 3):
+        open_y(0, 1, 1, PACK + 1)
+        for i in range(2, PACK):
+            h_pass(1, i, 1)
+        for s in range(2, PACK):
             open_y(0, 1, s, PACK + s)
+        for s in range(PACK):
             base(0, 1, s, 1)
-        open_y(0, 1, 3, PACK + 3)
-        cast_y(vector, 0, 0, 0, 3 * STRIP)
-        for i in range(PACK):
-            drain_h(vector if i % 2 else scalar, 1, i)
-        cast_y(scalar, 0, 0, 3 * STRIP, HALF)
+        cast_y(scalar, 0, 0, *strip(0))
+        drain_h(scalar, 1, 0)
+        drain_h(scalar, 1, 1)
+        cast_y(vector, 0, 0, STRIP, 3 * STRIP)
+        drain_h(scalar, 1, 2)
+        drain_h(scalar, 1, 3)
+        cast_y(vector, 0, 0, *strip(3))
         quant_h(1, 0, HALF // 2)
-        quant_h(1, HALF // 2, HALF)
         quant_y(0, 0)
         store_codes(0, 0)
+        cast_y(vector, 1, 0, *strip(0))
+        quant_h(1, HALF // 2, HALF)
         cast_y(scalar, 1, 0, Y_CUT, HALF)
+        open_y(1, 1, 0, 0)
         for s in range(PACK):
-            if s == 1:
-                base(0, 1, 3, 1)
             branch(0, 1, s)
-            drain(scalar if s else vector, 0, 1, s)
-        cast_y(vector, 1, 0, 0, Y_CUT)
-        quant_y(1, 0, Y_CUT, HALF)
+        cast_y(vector, 1, 0, *strip(1))
         quant_y(1, 0, 0, Y_CUT)
+        quant_y(1, 0, Y_CUT, HALF)
+        store_codes(1, 0)
+        for s in range(PACK):
+            drain(vector if s % 2 else scalar, 0, 1, s)
         for s in range(PACK):
             store_y(0, 1, s, 1)
-            if s == 2:
-                store_codes(1, 0)
         store_scales(0)
-        open_y(1, 1, 0, 0)
-        base(1, 1, 0, 1)
-        branch(1, 1, 0)
-        for s in range(1, PACK):
-            open_y(1, 1, s, s)
+        for s in range(PACK):
+            if s:
+                open_y(1, 1, s, s)
             base(1, 1, s, 1)
             branch(1, 1, s)
-        cast_y(vector, 0, 1)
+        for part in parts:
+            cast_y(vector, 0, 1, *part)
         drain(scalar, 1, 1, 0)
         drain(scalar, 1, 1, 1)
-        quant_y(0, 1)
+        for part in parts:
+            quant_y(0, 1, *part)
         store_y(1, 1, 0)
         store_codes(0, 1)
         drain(scalar, 1, 1, 2)

@@ -138,6 +138,31 @@ def tile_mix_lowrank_fm_pl_none_kernel(tc, x, w4_words, w4_scales, down, up, out
                                 rhs=h_codes[c][:].bitcast(FP8X4), rhs_scale=h_scales[c][:],
                                 start=False, stop=True)
 
+        def narrow_base(a, c, lo, hi, g, bank=None):
+            if g == 0:
+                y_acc[a, c, lo, hi] = ps.tile([P, 2, hi - lo], F32, name="bank%d" % bank)
+            for s in (2, 3):
+                col = a * SPAN + s * P
+                for at in range(lo, hi, STRIP):
+                    nc.tensor.matmul_mx(out=y_acc[a, c, lo, hi][:, s - 2, at - lo:at - lo + STRIP],
+                                        lhsT=w4_dealt[:, g, 2 * col:2 * (col + P)].bitcast(FP4X4),
+                                        lhsT_scale=s4_dealt[:, g, col:col + P],
+                                        rhs=x_codes[g, c][:, at:at + STRIP].bitcast(FP8X4),
+                                        rhs_scale=x_scales[g, c][:, at:at + STRIP],
+                                        start=(g == 0 and s == 2 and at == lo), stop=False)
+
+        def narrow_branch(a, c, lo, hi):
+            name = "up%d" % a
+            for s in (2, 3):
+                nc.tensor.matmul_mx(out=y_acc[a, c, lo, hi][:, s - 2, :],
+                                    lhsT=w_codes[name][:, s * P:(s + 1) * P].bitcast(FP8X4),
+                                    lhsT_scale=w_scales[name][:, s * P:(s + 1) * P],
+                                    rhs=h_codes[c][:, lo:hi].bitcast(FP8X4), rhs_scale=h_scales[c][:, lo:hi],
+                                    start=False, stop=(s == 3))
+
+        def narrow_drain(engine, a, c, lo, hi):
+            copy(engine, y_f32[a, c][:, 2:, lo:hi], y_acc[a, c, lo, hi][:])
+
         def h_pass(c, i, g, bank=None):
             cols = slice(*strip(i))
             if g == 0:
@@ -156,19 +181,19 @@ def tile_mix_lowrank_fm_pl_none_kernel(tc, x, w4_words, w4_scales, down, up, out
         def drain(engine, a, c, s, lo=0, hi=HALF):
             copy(engine, y_f32[a, c][:, s, lo:hi], y_acc[a, c, s][:, lo:hi])
 
-        def store_y(a, c, s, count=2):
+        def store_y(a, c, s, count=2, lo=0, hi=HALF):
             rows = out_0[a * SPAN:(a + 1) * SPAN, c * HALF:(c + 1) * HALF].rearrange("(p s) t -> p s t", s=PACK)
-            nc.sync.dma_start(out=rows[:, s:s + count, :], in_=y_f32[a, c][:, s:s + count, :])
+            nc.sync.dma_start(out=rows[:, s:s + count, lo:hi], in_=y_f32[a, c][:, s:s + count, lo:hi])
 
-        def store_codes(a, c):
+        def store_codes(a, c, lo=0, hi=HALF):
             words = out_1[a].rearrange("p t j -> p (t j)").bitcast(I32)
-            nc.sync.dma_start(out=words[:, c * HALF:(c + 1) * HALF], in_=y_codes[a, c][:].bitcast(I32))
+            nc.sync.dma_start(out=words[:, c * HALF + lo:c * HALF + hi], in_=y_codes[a, c][:, lo:hi].bitcast(I32))
 
-        def store_scales(c):
+        def store_scales(c, queue=nc.sync):
             for quad in range(PACK):
                 rows = out_2[:, 4 * quad:4 * quad + 4, c * HALF:(c + 1) * HALF].rearrange("a q t -> q a t")
-                nc.sync.dma_start(out=rows.bitcast(I32),
-                                  in_=y_scales[c][QUAD * quad:QUAD * quad + 4, :, :].bitcast(I32))
+                queue.dma_start(out=rows.bitcast(I32),
+                                in_=y_scales[c][QUAD * quad:QUAD * quad + 4, :, :].bitcast(I32))
 
         def deal_words(a):
             cols = slice(a * SPAN, (a + 1) * SPAN)
@@ -272,70 +297,101 @@ def tile_mix_lowrank_fm_pl_none_kernel(tc, x, w4_words, w4_scales, down, up, out
             if s % 2:
                 store_y(1, 0, s - 1)
 
-        for g in range(2):
-            for pair in ((0, 1), (2, 3)):
-                for i in pair:
-                    cast_x(vector, g, 1, *strip(i))
-                for i in pair:
-                    quant_x(g, 1, *strip(i))
-        for i in range(PACK):
+        left, right = parts
+        for i in (0, 1):
+            cast_x(vector, 0, 1, *strip(i))
+        for i in (0, 1):
+            quant_x(0, 1, *strip(i))
+        for i in (2, 3):
+            cast_x(vector, 0, 1, *strip(i))
+        quant_x(0, 1, *strip(2))
+        cast_y(vector, 0, 0, *strip(0))
+        quant_x(0, 1, *strip(3))
+        for i in (0, 1):
+            cast_x(vector, 1, 1, *strip(i))
+        for i in (0, 1):
+            quant_x(1, 1, *strip(i))
+        for i in (2, 3):
+            cast_x(vector, 1, 1, *strip(i))
+        quant_x(1, 1, *strip(2))
+        cast_y(vector, 0, 0, *strip(1))
+        quant_x(1, 1, *strip(3))
+        for i in (0, 1):
             h_pass(1, i, 0, i)
-        open_y(0, 1, 0, PACK)
-        for i in range(2):
+        for a in range(2):
+            narrow_base(a, 1, *left, 0, 2 + a)
+        for i in (2, 3):
+            h_pass(1, i, 0, 2 + i)
+        for i in (0, 1):
             h_pass(1, i, 1)
-        open_y(0, 1, 1, PACK + 1)
-        for i in range(2, PACK):
+        for a in range(2):
+            narrow_base(a, 1, *left, 1)
+        open_y(0, 1, 0, 6)
+        for i in (2, 3):
             h_pass(1, i, 1)
-        for s in range(2, PACK):
-            open_y(0, 1, s, PACK + s)
-        for s in range(PACK):
+        open_y(0, 1, 1, 7)
+        for s in range(2):
             base(0, 1, s, 1)
-        cast_y(scalar, 0, 0, *strip(0))
+        cast_y(scalar, 0, 0, *strip(3))
+        cast_y(scalar, 1, 0, *strip(3))
         drain_h(scalar, 1, 0)
         drain_h(scalar, 1, 1)
-        cast_y(vector, 0, 0, STRIP, 3 * STRIP)
-        drain_h(scalar, 1, 2)
-        drain_h(scalar, 1, 3)
-        cast_y(vector, 0, 0, *strip(3))
-        quant_h(1, 0, HALF // 2)
+        cast_y(vector, 0, 0, *strip(2))
+        cast_y(vector, 1, 0, *strip(2))
         quant_y(0, 0)
         store_codes(0, 0)
+        quant_h(1, *left)
+        cast_y(scalar, 1, 0, *strip(1))
+        drain_h(scalar, 1, 2)
+        drain_h(scalar, 1, 3)
         cast_y(vector, 1, 0, *strip(0))
-        quant_h(1, HALF // 2, HALF)
-        cast_y(scalar, 1, 0, Y_CUT, HALF)
-        open_y(1, 1, 0, 0)
-        for s in range(PACK):
-            branch(0, 1, s)
-        cast_y(vector, 1, 0, *strip(1))
-        quant_y(1, 0, 0, Y_CUT)
-        quant_y(1, 0, Y_CUT, HALF)
+        quant_y(1, 0, *right)
+        quant_y(1, 0, *left)
         store_codes(1, 0)
-        for s in range(PACK):
-            drain(vector if s % 2 else scalar, 0, 1, s)
-        for s in range(PACK):
-            store_y(0, 1, s, 1)
         store_scales(0)
-        for s in range(PACK):
-            if s:
-                open_y(1, 1, s, s)
-            base(1, 1, s, 1)
-            branch(1, 1, s)
+        for a in range(2):
+            narrow_branch(a, 1, *left)
+            narrow_drain(scalar, a, 1, *left)
+            store_y(a, 1, 2, 2, *left)
+        quant_h(1, *right)
+        for g in range(2):
+            narrow_base(0, 1, *right, g, 0)
+        open_y(1, 1, 0, 1)
+        for s in range(2):
+            branch(0, 1, s)
+        narrow_branch(0, 1, *right)
+        drain(vector, 0, 1, 0)
+        drain(scalar, 0, 1, 1)
+        narrow_drain(scalar, 0, 1, *right)
+        store_y(0, 1, 0, 1)
+        store_y(0, 1, 1, 1)
+        store_y(0, 1, 2, 2, *right)
+        base(1, 1, 0, 1)
+        branch(1, 1, 0)
+        open_y(1, 1, 1, 4)
+        base(1, 1, 1, 1)
+        branch(1, 1, 1)
+        for i in (2, 3):
+            for g in range(2):
+                narrow_base(1, 1, *strip(i), g, (5, 2)[i - 2])
+            narrow_branch(1, 1, *strip(i))
         for part in parts:
             cast_y(vector, 0, 1, *part)
-        drain(scalar, 1, 1, 0)
-        drain(scalar, 1, 1, 1)
         for part in parts:
             quant_y(0, 1, *part)
-        store_y(1, 1, 0)
+        for s in range(2):
+            drain(scalar, 1, 1, s)
+            store_y(1, 1, s, 1)
         store_codes(0, 1)
-        drain(scalar, 1, 1, 2)
-        drain(scalar, 1, 1, 3, 0, HALF // 2)
-        drain(scalar, 1, 1, 3, HALF // 2, HALF)
-        store_y(1, 1, 2)
-        cast_y(vector, 1, 1, 0, HALF // 2)
+        for i in (2, 3):
+            narrow_drain(scalar, 1, 1, *strip(i))
+        store_y(1, 1, 2, 2, *right)
+        cast_y(vector, 1, 1, *left)
         cast_y(vector, 1, 1, *strip(2))
         cast_y(scalar, 1, 1, *strip(3))
-        quant_y(1, 1, 0, HALF // 2)
-        quant_y(1, 1, HALF // 2, HALF)
-        store_codes(1, 1)
+        quant_y(1, 1, *left)
+        store_codes(1, 1, *left)
+        quant_y(1, 1, *strip(2))
+        quant_y(1, 1, *strip(3))
+        store_codes(1, 1, *right)
         store_scales(1)

@@ -48,8 +48,8 @@ def tile_mix_lowrank_fm_pl_none_kernel(tc, x, w4_words, w4_scales, down, up, out
         w_bf = {name: sbuf(name + "_bf", [P, PACK, P, PACK], BF16) for name in pieces}
         w_codes = {name: sbuf(name + "_codes", [P, SPAN], U32) for name in pieces}
         w_scales = {name: sbuf(name + "_scales", [P, SPAN], U8) for name in pieces}
-        w4_raw = sbuf("w4_raw", [P, 2, 2 * M], U8)
-        w4_dealt = sbuf("w4_dealt", [P, 2, 2 * M], U8)
+        w4_raw = [sbuf("w4_raw%d" % a, [P, 2, 2 * SPAN], U8) for a in range(2)]
+        w4_dealt = [sbuf("w4_dealt%d" % a, [P, 2, 2 * SPAN], U8) for a in range(2)]
         s4_raw = sbuf("s4_raw", [P, 2, M], U8)
         s4_dealt = sbuf("s4_dealt", [P, 2, M], U8)
         h_bf = [sbuf("h_bf%d" % c, [P, HALF, PACK], BF16) for c in range(2)]
@@ -121,7 +121,7 @@ def tile_mix_lowrank_fm_pl_none_kernel(tc, x, w4_words, w4_scales, down, up, out
         def base(a, c, s, g):
             col = a * SPAN + s * P
             nc.tensor.matmul_mx(out=y_acc[a, c, s][:],
-                                lhsT=w4_dealt[:, g, 2 * col:2 * (col + P)].bitcast(FP4X4),
+                                lhsT=w4_dealt[a][:, g, 2 * s * P:2 * (s + 1) * P].bitcast(FP4X4),
                                 lhsT_scale=s4_dealt[:, g, col:col + P],
                                 rhs=x_codes[g, c][:].bitcast(FP8X4), rhs_scale=x_scales[g, c][:],
                                 start=(g == 0), stop=False)
@@ -145,7 +145,7 @@ def tile_mix_lowrank_fm_pl_none_kernel(tc, x, w4_words, w4_scales, down, up, out
                 col = a * SPAN + s * P
                 for at in range(lo, hi, STRIP):
                     nc.tensor.matmul_mx(out=y_acc[a, c, lo, hi][:, s - 2, at - lo:at - lo + STRIP],
-                                        lhsT=w4_dealt[:, g, 2 * col:2 * (col + P)].bitcast(FP4X4),
+                                        lhsT=w4_dealt[a][:, g, 2 * s * P:2 * (s + 1) * P].bitcast(FP4X4),
                                         lhsT_scale=s4_dealt[:, g, col:col + P],
                                         rhs=x_codes[g, c][:, at:at + STRIP].bitcast(FP8X4),
                                         rhs_scale=x_scales[g, c][:, at:at + STRIP],
@@ -196,16 +196,16 @@ def tile_mix_lowrank_fm_pl_none_kernel(tc, x, w4_words, w4_scales, down, up, out
                                 in_=y_scales[c][QUAD * quad:QUAD * quad + 4, :, :].bitcast(I32))
 
         def deal_words(a):
-            cols = slice(a * SPAN, (a + 1) * SPAN)
-            vector.tensor_copy(out=w4_dealt[:].bitcast(U16)[:, :, cols].rearrange("p g (s m) -> p g s m", s=PACK),
-                               in_=w4_raw[:].bitcast(U16)[:, :, cols].rearrange("p g (m s) -> p g s m", s=PACK))
+            vector.tensor_copy(out=w4_dealt[a][:].bitcast(U16).rearrange("p g (s m) -> p g s m", s=PACK),
+                               in_=w4_raw[a][:].bitcast(U16).rearrange("p g (m s) -> p g s m", s=PACK))
 
         def deal_scales(g):
             vector.tensor_copy(out=s4_dealt[:, g, :].rearrange("p (a s m) -> p a s m", a=2, s=PACK),
                                in_=s4_raw[:, g, :].rearrange("p (a m s) -> p a s m", a=2, s=PACK))
 
-        def load_words():
-            nc.sync.dma_start(out=w4_raw[:].bitcast(I32), in_=w4_words.rearrange("g p b -> p g b").bitcast(I32))
+        def load_words(a):
+            words = w4_words.rearrange("g p b -> p g b")[:, :, 2 * a * SPAN:2 * (a + 1) * SPAN]
+            nc.sync.dma_start(out=w4_raw[a][:].bitcast(I32), in_=words.bitcast(I32))
 
         def load_scales():
             for quad in range(PACK):
@@ -214,30 +214,31 @@ def tile_mix_lowrank_fm_pl_none_kernel(tc, x, w4_words, w4_scales, down, up, out
 
         vector.memset(s4_raw[:].rearrange("p g n -> p (g n)").bitcast(I32), 0)
         parts = ((0, HALF // 2), (HALF // 2, HALF))
+        left, right = parts
         first, second = slice(0, 2), slice(2, PACK)
-        load_words()
-        load_scales()
+        load_words(0)
         load_x(0, 0)
+        load_scales()
         load_w("down0")
         load_w("down1")
         for part in parts:
             load_x(1, 0, *part)
+        load_words(1)
         for name in ("up0", "up1"):
             for part in parts:
                 load_w(name, *part)
-        for g in range(2):
-            for part in parts:
+        for part in parts:
+            for g in range(2):
                 load_x(g, 1, *part)
 
-        for a in range(2):
-            deal_words(a)
+        deal_words(0)
+        cast_x(scalar, 0, 0, *strip(3))
+        cast_x(vector, 0, 0, *left)
+        cast_x(vector, 0, 0, *strip(2))
+        quant_x(0, 0, *left)
+        quant_x(0, 0, *right)
         for g in range(2):
             deal_scales(g)
-        cast_x(scalar, 0, 0, *strip(3))
-        cast_x(vector, 0, 0, *parts[0])
-        cast_x(vector, 0, 0, *strip(2))
-        quant_x(0, 0, *parts[0])
-        quant_x(0, 0, *parts[1])
         for s in range(PACK):
             open_y(0, 0, s, s)
         for name in ("down0", "down1"):
@@ -257,31 +258,36 @@ def tile_mix_lowrank_fm_pl_none_kernel(tc, x, w4_words, w4_scales, down, up, out
         quant_x(1, 0, *strip(1))
         quant_x(1, 0, *strip(2))
         quant_x(1, 0, *strip(3))
+        deal_words(1)
         for i in range(PACK):
             h_pass(0, i, 1)
         for s in range(PACK):
             base(0, 0, s, 1)
         drain_h(scalar, 0, 0)
         drain_h(scalar, 0, 1)
-        cast_w(vector, "up0", 0, P // 2)
         drain_h(vector, 0, 2)
-        drain_h(vector, 0, 3)
-        cast_w(scalar, "up0", P // 2, P, first)
-        cast_w(scalar, "up0", P // 2, P, second)
-        quant_h(0, 0, HALF // 2)
-        quant_h(0, HALF // 2, HALF)
+        drain_h(scalar, 0, 3)
+        cast_w(scalar, "up0", 0, P // 2, first)
+        cast_w(scalar, "up0", 0, P // 2, second)
+        quant_h(0, *left)
+        cast_w(vector, "up0", P // 2, P, first)
+        quant_h(0, *right)
         quant_w("up0", 0, SPAN // 2)
+        cast_w(vector, "up0", P // 2, P, second)
+        cast_w(scalar, "up1", 0, P // 2, first)
+        cast_w(vector, "up1", 0, P // 2, second)
         quant_w("up0", SPAN // 2, SPAN)
         for s in range(2):
             open_y(1, 0, s, PACK + s)
             base(1, 0, s, 1)
-        cast_w(scalar, "up1", 0, P // 2, first)
-        cast_w(vector, "up1", 0, P // 2, second)
-        for s in range(PACK):
+        open_y(1, 0, 2, PACK + 2)
+        for s in range(2):
             branch(0, 0, s)
+        base(1, 0, 2, 1)
         for s in range(2, PACK):
-            open_y(1, 0, s, PACK + s)
-            base(1, 0, s, 1)
+            branch(0, 0, s)
+        open_y(1, 0, 3, PACK + 3)
+        base(1, 0, 3, 1)
         cast_w(vector, "up1", P // 2, P, first)
         cast_w(vector, "up1", P // 2, P, second)
         quant_w("up1", 0, SPAN // 2)
@@ -297,80 +303,70 @@ def tile_mix_lowrank_fm_pl_none_kernel(tc, x, w4_words, w4_scales, down, up, out
             if s % 2:
                 store_y(1, 0, s - 1)
 
-        left, right = parts
-        for i in (0, 1):
+        for g in range(2):
+            for i in (0, 1):
+                cast_x(vector, g, 1, *strip(i))
+            for i in (0, 1):
+                quant_x(g, 1, *strip(i))
+        for i in (2, 3):
             cast_x(vector, 0, 1, *strip(i))
-        for i in (0, 1):
+        for i in (2, 3):
             quant_x(0, 1, *strip(i))
         for i in (2, 3):
-            cast_x(vector, 0, 1, *strip(i))
-        quant_x(0, 1, *strip(2))
-        cast_y(vector, 0, 0, *strip(0))
-        quant_x(0, 1, *strip(3))
-        for i in (0, 1):
             cast_x(vector, 1, 1, *strip(i))
-        for i in (0, 1):
-            quant_x(1, 1, *strip(i))
         for i in (2, 3):
-            cast_x(vector, 1, 1, *strip(i))
-        quant_x(1, 1, *strip(2))
-        cast_y(vector, 0, 0, *strip(1))
-        quant_x(1, 1, *strip(3))
+            quant_x(1, 1, *strip(i))
         for i in (0, 1):
             h_pass(1, i, 0, i)
-        for a in range(2):
-            narrow_base(a, 1, *left, 0, 2 + a)
-        for i in (2, 3):
-            h_pass(1, i, 0, 2 + i)
+        narrow_base(0, 1, *left, 0, 2)
         for i in (0, 1):
             h_pass(1, i, 1)
-        for a in range(2):
-            narrow_base(a, 1, *left, 1)
-        open_y(0, 1, 0, 6)
+        narrow_base(0, 1, *left, 1)
+        for i in (2, 3):
+            h_pass(1, i, 0, 2 + i)
+        narrow_base(1, 1, *left, 0, 3)
         for i in (2, 3):
             h_pass(1, i, 1)
-        open_y(0, 1, 1, 7)
-        for s in range(2):
-            base(0, 1, s, 1)
+        for i in (0, 1):
+            drain_h(scalar, 1, i)
         cast_y(scalar, 0, 0, *strip(3))
-        cast_y(scalar, 1, 0, *strip(3))
-        drain_h(scalar, 1, 0)
-        drain_h(scalar, 1, 1)
-        cast_y(vector, 0, 0, *strip(2))
-        cast_y(vector, 1, 0, *strip(2))
+        for i in (2, 3):
+            drain_h(scalar, 1, i)
+        cast_y(vector, 0, 0, *strip(0))
+        quant_h(1, *left)
+        cast_y(vector, 0, 0, STRIP, 3 * STRIP)
+        cast_y(vector, 1, 0, *strip(0))
         quant_y(0, 0)
         store_codes(0, 0)
-        quant_h(1, *left)
-        cast_y(scalar, 1, 0, *strip(1))
-        drain_h(scalar, 1, 2)
-        drain_h(scalar, 1, 3)
-        cast_y(vector, 1, 0, *strip(0))
-        quant_y(1, 0, *right)
-        quant_y(1, 0, *left)
-        store_codes(1, 0)
-        store_scales(0)
+        quant_h(1, *right)
+        narrow_base(1, 1, *left, 1)
         for a in range(2):
             narrow_branch(a, 1, *left)
             narrow_drain(scalar, a, 1, *left)
             store_y(a, 1, 2, 2, *left)
-        quant_h(1, *right)
-        for g in range(2):
-            narrow_base(0, 1, *right, g, 0)
-        open_y(1, 1, 0, 1)
+        for s in range(2):
+            open_y(0, 1, s, 6 + s)
+            base(0, 1, s, 1)
         for s in range(2):
             branch(0, 1, s)
+        cast_y(vector, 1, 0, *strip(1))
+        cast_y(vector, 1, 0, *right)
+        quant_y(1, 0, *left)
+        quant_y(1, 0, *right)
+        for g in range(2):
+            narrow_base(0, 1, *right, g, 0)
         narrow_branch(0, 1, *right)
-        drain(vector, 0, 1, 0)
-        drain(scalar, 0, 1, 1)
+        drain(scalar, 0, 1, 0)
+        drain(vector, 0, 1, 1)
         narrow_drain(scalar, 0, 1, *right)
-        store_y(0, 1, 0, 1)
-        store_y(0, 1, 1, 1)
+        store_codes(1, 0)
+        store_scales(0)
+        store_y(0, 1, 0)
         store_y(0, 1, 2, 2, *right)
-        base(1, 1, 0, 1)
-        branch(1, 1, 0)
-        open_y(1, 1, 1, 4)
-        base(1, 1, 1, 1)
-        branch(1, 1, 1)
+        for s in range(2):
+            open_y(1, 1, s, (1, 4)[s])
+            base(1, 1, s, 1)
+            branch(1, 1, s)
         for i in (2, 3):
             for g in range(2):
                 narrow_base(1, 1, *strip(i), g, (5, 2)[i - 2])
@@ -387,11 +383,9 @@ def tile_mix_lowrank_fm_pl_none_kernel(tc, x, w4_words, w4_scales, down, up, out
             narrow_drain(scalar, 1, 1, *strip(i))
         store_y(1, 1, 2, 2, *right)
         cast_y(vector, 1, 1, *left)
-        cast_y(vector, 1, 1, *strip(2))
-        cast_y(scalar, 1, 1, *strip(3))
-        quant_y(1, 1, *left)
-        store_codes(1, 1, *left)
-        quant_y(1, 1, *strip(2))
-        quant_y(1, 1, *strip(3))
-        store_codes(1, 1, *right)
+        for i in (2, 3):
+            cast_y(vector, 1, 1, *strip(i))
+        for part in parts:
+            quant_y(1, 1, *part)
+            store_codes(1, 1, *part)
         store_scales(1)

@@ -163,12 +163,12 @@ def tile_mix_lowrank_fm_pl_none_kernel(tc, x, w4_words, w4_scales, down, up, out
         def narrow_drain(engine, a, c, lo, hi):
             copy(engine, y_f32[a, c][:, 2:, lo:hi], y_acc[a, c, lo, hi][:])
 
-        def h_pass(c, i, g, bank=None):
+        def h_pass(c, i, g, bank=None, slots=range(PACK)):
             cols = slice(*strip(i))
-            if g == 0:
+            if bank is not None:
                 h_acc[c, i] = ps.tile([P, PACK, STRIP], F32, name="bank%d" % bank)
             name = "down%d" % g
-            for s in range(PACK):
+            for s in slots:
                 nc.tensor.matmul_mx(out=h_acc[c, i][:, s, :],
                                     lhsT=w_codes[name][:, s * P:(s + 1) * P].bitcast(FP8X4),
                                     lhsT_scale=w_scales[name][:, s * P:(s + 1) * P],
@@ -237,19 +237,23 @@ def tile_mix_lowrank_fm_pl_none_kernel(tc, x, w4_words, w4_scales, down, up, out
         cast_x(vector, 0, 0, *strip(2))
         quant_x(0, 0, *left)
         quant_x(0, 0, *right)
-        for g in range(2):
-            deal_scales(g)
+        deal_scales(0)
         for s in range(PACK):
             open_y(0, 0, s, s)
-        for name in ("down0", "down1"):
-            cast_w(scalar, name, 0, P, slice(3, PACK))
-            cast_w(vector, name, 0, P, first)
-            cast_w(vector, name, 0, P, slice(2, 3))
-            quant_w(name, 0, SPAN // 2)
-            quant_w(name, SPAN // 2, SPAN)
-            if name == "down0":
-                for i in range(PACK):
-                    h_pass(0, i, 0, PACK + i)
+        cast_w(vector, "down0", 0, P, first)
+        cast_w(scalar, "down0", 0, P, second)
+        deal_scales(1)
+        quant_w("down0", 0, SPAN // 2)
+        for i in range(PACK):
+            h_pass(0, i, 0, PACK + i, (0, 1))
+        cast_w(vector, "down1", 0, P, first)
+        cast_w(scalar, "down1", UP_CUT, P, second)
+        quant_w("down0", SPAN // 2, SPAN)
+        for i in range(PACK):
+            h_pass(0, i, 0, None, (2, 3))
+        cast_w(vector, "down1", 0, UP_CUT, second)
+        quant_w("down1", 0, SPAN // 2)
+        quant_w("down1", SPAN // 2, SPAN)
         cast_x(scalar, 1, 0, *strip(0))
         cast_x(vector, 1, 0, *strip(1))
         quant_x(1, 0, *strip(0))

@@ -48,7 +48,7 @@ def tile_mix_lowrank_fm_pl_none_kernel(tc, x, w4_words, w4_scales, down, up, out
         w_bf = {name: sbuf(name + "_bf", [P, PACK, P, PACK], BF16) for name in pieces}
         w_codes = {name: sbuf(name + "_codes", [P, SPAN], U32) for name in pieces}
         w_scales = {name: sbuf(name + "_scales", [P, SPAN], U8) for name in pieces}
-        w4_raw = [sbuf("w4_raw%d" % a, [P, 2, 2 * SPAN], U8) for a in range(2)]
+        w4_raw = {}
         w4_dealt = [sbuf("w4_dealt%d" % a, [P, 2, 2 * SPAN], U8) for a in range(2)]
         s4_raw = sbuf("s4_raw", [P, 2, M], U8)
         s4_dealt = sbuf("s4_dealt", [P, 2, M], U8)
@@ -195,17 +195,20 @@ def tile_mix_lowrank_fm_pl_none_kernel(tc, x, w4_words, w4_scales, down, up, out
                 queue.dma_start(out=rows.bitcast(I32),
                                 in_=y_scales[c][QUAD * quad:QUAD * quad + 4, :, :].bitcast(I32))
 
-        def deal_words(a):
-            vector.tensor_copy(out=w4_dealt[a][:].bitcast(U16).rearrange("p g (s m) -> p g s m", s=PACK),
-                               in_=w4_raw[a][:].bitcast(U16).rearrange("p g (m s) -> p g s m", s=PACK))
+        def deal_words(a, g):
+            at = a if (g, a) in w4_raw else 0
+            words = w4_raw[g, at][:, 2 * (a - at) * SPAN:2 * (a - at + 1) * SPAN]
+            vector.tensor_copy(out=w4_dealt[a][:, g, :].bitcast(U16).rearrange("p (s m) -> p s m", s=PACK),
+                               in_=words.bitcast(U16).rearrange("p (m s) -> p s m", s=PACK))
 
         def deal_scales(g):
             vector.tensor_copy(out=s4_dealt[:, g, :].rearrange("p (a s m) -> p a s m", a=2, s=PACK),
                                in_=s4_raw[:, g, :].rearrange("p (a m s) -> p a s m", a=2, s=PACK))
 
-        def load_words(a):
-            words = w4_words.rearrange("g p b -> p g b")[:, :, 2 * a * SPAN:2 * (a + 1) * SPAN]
-            nc.sync.dma_start(out=w4_raw[a][:].bitcast(I32), in_=words.bitcast(I32))
+        def load_words(g, lo, hi):
+            w4_raw[g, lo] = sbuf("w4_raw%d%d" % (g, lo), [P, 2 * (hi - lo) * SPAN], U8)
+            nc.sync.dma_start(out=w4_raw[g, lo][:].bitcast(I32),
+                              in_=w4_words[g, :, 2 * lo * SPAN:2 * hi * SPAN].bitcast(I32))
 
         def load_scales():
             for quad in range(PACK):
@@ -216,14 +219,15 @@ def tile_mix_lowrank_fm_pl_none_kernel(tc, x, w4_words, w4_scales, down, up, out
         parts = ((0, HALF // 2), (HALF // 2, HALF))
         left, right = parts
         first, second = slice(0, 2), slice(2, PACK)
-        load_words(0)
+        load_words(0, 0, 1)
         load_x(0, 0)
         load_scales()
         load_w("down0")
         load_w("down1")
         for part in parts:
             load_x(1, 0, *part)
-        load_words(1)
+        load_words(1, 0, 2)
+        load_words(0, 1, 2)
         for name in ("up0", "up1"):
             for part in parts:
                 load_w(name, *part)
@@ -231,7 +235,7 @@ def tile_mix_lowrank_fm_pl_none_kernel(tc, x, w4_words, w4_scales, down, up, out
             for g in range(2):
                 load_x(g, 1, *part)
 
-        deal_words(0)
+        deal_words(0, 0)
         cast_x(scalar, 0, 0, *strip(3))
         cast_x(vector, 0, 0, *left)
         cast_x(vector, 0, 0, *strip(2))
@@ -262,22 +266,21 @@ def tile_mix_lowrank_fm_pl_none_kernel(tc, x, w4_words, w4_scales, down, up, out
         quant_x(1, 0, *strip(1))
         quant_x(1, 0, *strip(2))
         quant_x(1, 0, *strip(3))
-        deal_words(1)
+        deal_words(0, 1)
+        deal_words(1, 0)
         for i in range(PACK):
             h_pass(0, i, 1)
         for s in range(PACK):
             base(0, 0, s, 1)
-        drain_h(scalar, 0, 0)
-        drain_h(scalar, 0, 1)
-        drain_h(vector, 0, 2)
-        drain_h(scalar, 0, 3)
-        cast_w(scalar, "up0", 0, P // 2, first)
-        cast_w(scalar, "up0", 0, P // 2, second)
+        for i in range(PACK):
+            drain_h(scalar, 0, i)
+        deal_words(1, 1)
+        cast_w(vector, "up0", 0, P // 2)
         quant_h(0, *left)
         cast_w(vector, "up0", P // 2, P, first)
+        cast_w(scalar, "up0", P // 2, P, second)
         quant_h(0, *right)
         quant_w("up0", 0, SPAN // 2)
-        cast_w(vector, "up0", P // 2, P, second)
         cast_w(scalar, "up1", 0, P // 2, first)
         cast_w(vector, "up1", 0, P // 2, second)
         quant_w("up0", SPAN // 2, SPAN)

from contextlib import ExitStack

import concourse.mybir as mybir

K, R, M, T = 1024, 512, 1024, 1024
FLOPS = 2 * T * (K * R + K * M + R * M)

F32 = mybir.dt.float32
BF16 = mybir.dt.bfloat16
I32 = mybir.dt.int32
U32 = mybir.dt.uint32
U16 = mybir.dt.uint16
U8 = mybir.dt.uint8
FP8X4 = mybir.dt.float8_e4m3fn_x4
FP4X4 = mybir.dt.float4_e2m1fn_x4

P = 128
PACK = 4
SPAN = P * PACK
HALF = 512
STRIP = 128
QUAD = 32

DEAL_CUT = 80
X_CUT = 384
UP_CUT = 32
Y_CUT = 256


def tile_mix_lowrank_fm_pl_none_kernel(tc, x, w4_words, w4_scales, down, up, out_0, out_1, out_2):
    nc = tc.nc
    scalar, vector = nc.scalar, nc.vector
    with ExitStack() as ctx:
        sb = ctx.enter_context(tc.tile_pool(name="sb", bufs=1))
        ps = ctx.enter_context(tc.psum_pool(name="ps", bufs=1))
        ctx.enter_context(tc.manual_schedule())

        def sbuf(name, shape, dtype):
            return sb.tile(shape, dtype, name=name, align_bytes=256)

        two_by_two = [(i, j) for i in range(2) for j in range(2)]
        x_raw = {}
        x_bf = {gc: sbuf("x_bf%d%d" % gc, [P, HALF, PACK], BF16) for gc in two_by_two}
        x_codes = {gc: sbuf("x_codes%d%d" % gc, [P, HALF], U32) for gc in two_by_two}
        x_scales = {gc: sbuf("x_scales%d%d" % gc, [P, HALF], U8) for gc in two_by_two}
        pieces = {"down0": down[:SPAN, :], "down1": down[SPAN:, :], "up0": up[:, :SPAN], "up1": up[:, SPAN:]}
        w_raw = {}
        w_bf = {name: sbuf(name + "_bf", [P, PACK, P, PACK], BF16) for name in pieces}
        w_codes = {name: sbuf(name + "_codes", [P, SPAN], U32) for name in pieces}
        w_scales = {name: sbuf(name + "_scales", [P, SPAN], U8) for name in pieces}
        w4_raw = {}
        w4_dealt = [sbuf("w4_dealt%d" % a, [P, 2, 2 * SPAN], U8) for a in range(2)]
        s4_raw = sbuf("s4_raw", [P, 2, M], U8)
        s4_dealt = sbuf("s4_dealt", [P, 2, M], U8)
        h_bf = [sbuf("h_bf%d" % c, [P, HALF, PACK], BF16) for c in range(2)]
        h_codes = [sbuf("h_codes%d" % c, [P, HALF], U32) for c in range(2)]
        h_scales = [sbuf("h_scales%d" % c, [P, HALF], U8) for c in range(2)]
        y_f32 = {ac: sbuf("y_f32%d%d" % ac, [P, PACK, HALF], F32) for ac in two_by_two}
        y_bf = {ac: sbuf("y_bf%d%d" % ac, [P, HALF, PACK], BF16) for ac in two_by_two}
        y_codes = {ac: sbuf("y_codes%d%d" % ac, [P, HALF], U32) for ac in two_by_two}
        y_scales = [sbuf("y_scales%d" % c, [P, 2, HALF], U8) for c in range(2)]
        y_acc = {}
        h_acc = {}

        def copy(engine, out, in_):
            if engine is scalar:
                scalar.copy(out=out, in_=in_)
            else:
                vector.tensor_copy(out=out, in_=in_)

        def load_x(g, c, lo=0, hi=HALF):
            rows = x[g * SPAN:(g + 1) * SPAN, c * HALF + lo:c * HALF + hi]
            x_raw[g, c, lo] = sbuf("x_raw%d%d_%d" % (g, c, lo), [P, PACK, hi - lo], F32)
            nc.sync.dma_start(out=x_raw[g, c, lo][:], in_=rows.rearrange("(p j) t -> p j t", j=PACK))

        def load_w(name, lo=0, hi=SPAN):
            w_raw[name, lo] = sbuf("%s_raw%d" % (name, lo), [P, PACK, hi - lo], F32)
            nc.sync.dma_start(out=w_raw[name, lo][:],
                              in_=pieces[name][:, lo:hi].rearrange("(p j) n -> p j n", j=PACK))

        def interleave(engine, dst, src):
            copy(engine, dst.rearrange("p (u i) j -> p u j i", i=4), src.rearrange("p j (u i) -> p u j i", i=4))

        def cast_x(engine, g, c, lo, hi):
            at = max(key[2] for key in x_raw if key[:2] == (g, c) and key[2] <= lo)
            interleave(engine, x_bf[g, c][:, lo:hi, :], x_raw[g, c, at][:, :, lo - at:hi - at])

        def cast_y(engine, a, c, lo=0, hi=HALF):
            interleave(engine, y_bf[a, c][:, lo:hi, :], y_f32[a, c][:, :, lo:hi])

        def cast_w(engine, name, lo, hi, slots=slice(0, PACK)):
            at = max(key[1] for key in w_raw if key[0] == name and key[1] <= PACK * lo)
            raw = w_raw[name, at][:, :, PACK * lo - at:PACK * hi - at]
            copy(engine,
                 w_bf[name][:, slots, lo:hi, :].rearrange("p s m j -> p m j s"),
                 raw.rearrange("p j (m s) -> p m j s", s=PACK)[:, :, :, slots])

        def cast_w_shared(name):
            cast_w(vector, name, 0, DEAL_CUT)
            cast_w(scalar, name, DEAL_CUT, P)

        def quantize(codes, scales, values, lo, hi):
            vector.quantize_mx(out=codes[:, lo:hi].bitcast(FP8X4), scales=scales[:, lo:hi],
                               in_=values[:, PACK * lo:PACK * hi])

        def quant_x(g, c, lo=0, hi=HALF):
            quantize(x_codes[g, c], x_scales[g, c], x_bf[g, c][:].rearrange("p t j -> p (t j)"), lo, hi)

        def quant_w(name, lo=0, hi=SPAN):
            quantize(w_codes[name], w_scales[name], w_bf[name][:].rearrange("p s m j -> p (s m j)"), lo, hi)

        def quant_h(c, lo, hi):
            quantize(h_codes[c], h_scales[c], h_bf[c][:].rearrange("p t j -> p (t j)"), lo, hi)

        def quant_y(a, c, lo=0, hi=HALF):
            quantize(y_codes[a, c], y_scales[c][:, a, :], y_bf[a, c][:].rearrange("p t j -> p (t j)"), lo, hi)

        def strip(i):
            return i * STRIP, (i + 1) * STRIP

        def base(a, c, s, g):
            col = a * SPAN + s * P
            nc.tensor.matmul_mx(out=y_acc[a, c, s][:],
                                lhsT=w4_dealt[a][:, g, 2 * s * P:2 * (s + 1) * P].bitcast(FP4X4),
                                lhsT_scale=s4_dealt[:, g, col:col + P],
                                rhs=x_codes[g, c][:].bitcast(FP8X4), rhs_scale=x_scales[g, c][:],
                                start=(g == 0), stop=False)

        def open_y(a, c, s, bank):
            y_acc[a, c, s] = ps.tile([P, HALF], F32, name="bank%d" % bank)
            base(a, c, s, 0)

        def branch(a, c, s):
            name = "up%d" % a
            nc.tensor.matmul_mx(out=y_acc[a, c, s][:],
                                lhsT=w_codes[name][:, s * P:(s + 1) * P].bitcast(FP8X4),
                                lhsT_scale=w_scales[name][:, s * P:(s + 1) * P],
                                rhs=h_codes[c][:].bitcast(FP8X4), rhs_scale=h_scales[c][:],
                                start=False, stop=True)

        def narrow_base(a, c, lo, hi, g, bank=None):
            if g == 0:
                y_acc[a, c, lo, hi] = ps.tile([P, 2, hi - lo], F32, name="bank%d" % bank)
            for s in (2, 3):
                col = a * SPAN + s * P
                for at in range(lo, hi, STRIP):
                    nc.tensor.matmul_mx(out=y_acc[a, c, lo, hi][:, s - 2, at - lo:at - lo + STRIP],
                                        lhsT=w4_dealt[a][:, g, 2 * s * P:2 * (s + 1) * P].bitcast(FP4X4),
                                        lhsT_scale=s4_dealt[:, g, col:col + P],
                                        rhs=x_codes[g, c][:, at:at + STRIP].bitcast(FP8X4),
                                        rhs_scale=x_scales[g, c][:, at:at + STRIP],
                                        start=(g == 0 and s == 2 and at == lo), stop=False)

        def narrow_branch(a, c, lo, hi):
            name = "up%d" % a
            for s in (2, 3):
                nc.tensor.matmul_mx(out=y_acc[a, c, lo, hi][:, s - 2, :],
                                    lhsT=w_codes[name][:, s * P:(s + 1) * P].bitcast(FP8X4),
                                    lhsT_scale=w_scales[name][:, s * P:(s + 1) * P],
                                    rhs=h_codes[c][:, lo:hi].bitcast(FP8X4), rhs_scale=h_scales[c][:, lo:hi],
                                    start=False, stop=(s == 3))

        def narrow_drain(engine, a, c, lo, hi):
            copy(engine, y_f32[a, c][:, 2:, lo:hi], y_acc[a, c, lo, hi][:])

        def h_pass(c, i, g, bank=None, slots=range(PACK)):
            cols = slice(*strip(i))
            if bank is not None:
                h_acc[c, i] = ps.tile([P, PACK, STRIP], F32, name="bank%d" % bank)
            name = "down%d" % g
            for s in slots:
                nc.tensor.matmul_mx(out=h_acc[c, i][:, s, :],
                                    lhsT=w_codes[name][:, s * P:(s + 1) * P].bitcast(FP8X4),
                                    lhsT_scale=w_scales[name][:, s * P:(s + 1) * P],
                                    rhs=x_codes[g, c][:, cols].bitcast(FP8X4), rhs_scale=x_scales[g, c][:, cols],
                                    start=(g == 0 and s == 0), stop=(g == 1 and s == PACK - 1))

        def drain_h(engine, c, i):
            copy(engine, h_bf[c][:, slice(*strip(i)), :], h_acc[c, i][:].rearrange("p s t -> p t s"))

        def drain(engine, a, c, s, lo=0, hi=HALF):
            copy(engine, y_f32[a, c][:, s, lo:hi], y_acc[a, c, s][:, lo:hi])

        def store_y(a, c, s, count=2, lo=0, hi=HALF):
            rows = out_0[a * SPAN:(a + 1) * SPAN, c * HALF:(c + 1) * HALF].rearrange("(p s) t -> p s t", s=PACK)
            nc.sync.dma_start(out=rows[:, s:s + count, lo:hi], in_=y_f32[a, c][:, s:s + count, lo:hi])

        def store_codes(a, c, lo=0, hi=HALF):
            words = out_1[a].rearrange("p t j -> p (t j)").bitcast(I32)
            nc.sync.dma_start(out=words[:, c * HALF + lo:c * HALF + hi], in_=y_codes[a, c][:, lo:hi].bitcast(I32))

        def store_scales(c, queue=nc.sync):
            for quad in range(PACK):
                rows = out_2[:, 4 * quad:4 * quad + 4, c * HALF:(c + 1) * HALF].rearrange("a q t -> q a t")
                queue.dma_start(out=rows.bitcast(I32),
                                in_=y_scales[c][QUAD * quad:QUAD * quad + 4, :, :].bitcast(I32))

        def deal_words(a, g):
            at = a if (g, a) in w4_raw else 0
            words = w4_raw[g, at][:, 2 * (a - at) * SPAN:2 * (a - at + 1) * SPAN]
            vector.tensor_copy(out=w4_dealt[a][:, g, :].bitcast(U16).rearrange("p (s m) -> p s m", s=PACK),
                               in_=words.bitcast(U16).rearrange("p (m s) -> p s m", s=PACK))

        def deal_scales(g):
            vector.tensor_copy(out=s4_dealt[:, g, :].rearrange("p (a s m) -> p a s m", a=2, s=PACK),
                               in_=s4_raw[:, g, :].rearrange("p (a m s) -> p a s m", a=2, s=PACK))

        def load_words(g, lo, hi):
            w4_raw[g, lo] = sbuf("w4_raw%d%d" % (g, lo), [P, 2 * (hi - lo) * SPAN], U8)
            nc.sync.dma_start(out=w4_raw[g, lo][:].bitcast(I32),
                              in_=w4_words[g, :, 2 * lo * SPAN:2 * hi * SPAN].bitcast(I32))

        def load_scales():
            for quad in range(PACK):
                nc.sync.dma_start(out=s4_raw[QUAD * quad:QUAD * quad + 4, :, :].bitcast(I32),
                                  in_=w4_scales[:, 4 * quad:4 * quad + 4, :].rearrange("g q n -> q g n").bitcast(I32))

        vector.memset(s4_raw[:].rearrange("p g n -> p (g n)").bitcast(I32), 0)
        parts = ((0, HALF // 2), (HALF // 2, HALF))
        left, right = parts
        first, second = slice(0, 2), slice(2, PACK)
        load_words(0, 0, 1)
        load_x(0, 0)
        load_scales()
        load_w("down0")
        load_w("down1")
        for part in parts:
            load_x(1, 0, *part)
        load_words(1, 0, 2)
        load_words(0, 1, 2)
        for name in ("up0", "up1"):
            for part in parts:
                load_w(name, *part)
        for part in parts:
            for g in range(2):
                load_x(g, 1, *part)

        deal_words(0, 0)
        cast_x(scalar, 0, 0, *strip(3))
        cast_x(vector, 0, 0, *left)
        cast_x(vector, 0, 0, *strip(2))
        quant_x(0, 0, *left)
        quant_x(0, 0, *right)
        deal_scales(0)
        for s in range(PACK):
            open_y(0, 0, s, s)
        cast_w(vector, "down0", 0, P, first)
        cast_w(scalar, "down0", 0, P, second)
        deal_scales(1)
        quant_w("down0", 0, SPAN // 2)
        for i in range(PACK):
            h_pass(0, i, 0, PACK + i, (0, 1))
        cast_w(vector, "down1", 0, P, first)
        cast_w(scalar, "down1", UP_CUT, P, second)
        quant_w("down0", SPAN // 2, SPAN)
        for i in range(PACK):
            h_pass(0, i, 0, None, (2, 3))
        cast_w(vector, "down1", 0, UP_CUT, second)
        quant_w("down1", 0, SPAN // 2)
        quant_w("down1", SPAN // 2, SPAN)
        cast_x(scalar, 1, 0, *strip(0))
        cast_x(vector, 1, 0, *strip(1))
        quant_x(1, 0, *strip(0))
        cast_x(scalar, 1, 0, *strip(3))
        cast_x(vector, 1, 0, *strip(2))
        quant_x(1, 0, *strip(1))
        quant_x(1, 0, *strip(2))
        quant_x(1, 0, *strip(3))
        deal_words(0, 1)
        deal_words(1, 0)
        for i in range(PACK):
            h_pass(0, i, 1)
        for s in range(PACK):
            base(0, 0, s, 1)
        for i in range(PACK):
            drain_h(scalar, 0, i)
        deal_words(1, 1)
        cast_w(vector, "up0", 0, P // 2)
        quant_h(0, *left)
        cast_w(vector, "up0", P // 2, P, first)
        cast_w(scalar, "up0", P // 2, P, second)
        quant_h(0, *right)
        quant_w("up0", 0, SPAN // 2)
        cast_w(scalar, "up1", 0, P // 2, first)
        cast_w(vector, "up1", 0, P // 2, second)
        quant_w("up0", SPAN // 2, SPAN)
        for s in range(2):
            open_y(1, 0, s, PACK + s)
            base(1, 0, s, 1)
        open_y(1, 0, 2, PACK + 2)
        for s in range(2):
            branch(0, 0, s)
        base(1, 0, 2, 1)
        for s in range(2, PACK):
            branch(0, 0, s)
        open_y(1, 0, 3, PACK + 3)
        base(1, 0, 3, 1)
        cast_w(vector, "up1", P // 2, P, first)
        cast_w(vector, "up1", P // 2, P, second)
        quant_w("up1", 0, SPAN // 2)
        quant_w("up1", SPAN // 2, SPAN)
        for s in range(PACK):
            drain(scalar, 0, 0, s)
            if s % 2:
                store_y(0, 0, s - 1)
        for s in range(PACK):
            branch(1, 0, s)
        for s in range(PACK):
            drain(scalar, 1, 0, s)
            if s % 2:
                store_y(1, 0, s - 1)

        for g in range(2):
            for i in (0, 1):
                cast_x(vector, g, 1, *strip(i))
            for i in (0, 1):
                quant_x(g, 1, *strip(i))
        for i in (2, 3):
            cast_x(vector, 0, 1, *strip(i))
        for i in (2, 3):
            quant_x(0, 1, *strip(i))
        for i in (2, 3):
            cast_x(vector, 1, 1, *strip(i))
        for i in (2, 3):
            quant_x(1, 1, *strip(i))
        for i in (0, 1):
            h_pass(1, i, 0, i)
        narrow_base(0, 1, *left, 0, 2)
        for i in (0, 1):
            h_pass(1, i, 1)
        narrow_base(0, 1, *left, 1)
        for i in (2, 3):
            h_pass(1, i, 0, 2 + i)
        narrow_base(1, 1, *left, 0, 3)
        for i in (2, 3):
            h_pass(1, i, 1)
        for i in (0, 1):
            drain_h(scalar, 1, i)
        cast_y(scalar, 0, 0, *strip(3))
        for i in (2, 3):
            drain_h(scalar, 1, i)
        cast_y(vector, 0, 0, *strip(0))
        quant_h(1, *left)
        cast_y(vector, 0, 0, STRIP, 3 * STRIP)
        cast_y(vector, 1, 0, *strip(0))
        quant_y(0, 0)
        store_codes(0, 0)
        quant_h(1, *right)
        narrow_base(1, 1, *left, 1)
        for a in range(2):
            narrow_branch(a, 1, *left)
            narrow_drain(scalar, a, 1, *left)
            store_y(a, 1, 2, 2, *left)
        for s in range(2):
            open_y(0, 1, s, 6 + s)
            base(0, 1, s, 1)
        for s in range(2):
            branch(0, 1, s)
        cast_y(vector, 1, 0, *strip(1))
        cast_y(vector, 1, 0, *right)
        quant_y(1, 0, *left)
        quant_y(1, 0, *right)
        for g in range(2):
            narrow_base(0, 1, *right, g, 0)
        narrow_branch(0, 1, *right)
        drain(scalar, 0, 1, 0)
        drain(vector, 0, 1, 1)
        narrow_drain(scalar, 0, 1, *right)
        store_codes(1, 0)
        store_scales(0)
        store_y(0, 1, 0)
        store_y(0, 1, 2, 2, *right)
        for s in range(2):
            open_y(1, 1, s, (1, 4)[s])
            base(1, 1, s, 1)
            branch(1, 1, s)
        for i in (2, 3):
            for g in range(2):
                narrow_base(1, 1, *strip(i), g, (5, 2)[i - 2])
            narrow_branch(1, 1, *strip(i))
        for part in parts:
            cast_y(vector, 0, 1, *part)
        for part in parts:
            quant_y(0, 1, *part)
        for s in range(2):
            drain(scalar, 1, 1, s)
            store_y(1, 1, s, 1)
        store_codes(0, 1)
        for i in (2, 3):
            narrow_drain(scalar, 1, 1, *strip(i))
        store_y(1, 1, 2, 2, *right)
        cast_y(vector, 1, 1, *left)
        for i in (2, 3):
            cast_y(vector, 1, 1, *strip(i))
        for part in parts:
            quant_y(1, 1, *part)
            store_codes(1, 1, *part)
        store_scales(1)
